import numpy as np
import ml_dtypes


def mxq(x, axis, fmt="e4m3"):
    dtype, down = {"e4m3": (ml_dtypes.float8_e4m3fn, 7), "e5m2": (ml_dtypes.float8_e5m2, 14)}[fmt]
    v = np.moveaxis(np.asarray(x, np.float32).astype(ml_dtypes.bfloat16).astype(np.float64), axis, -1)
    blocks = v.reshape(v.shape[:-1] + (-1, 32))
    amax = np.abs(blocks).max(-1, keepdims=True)
    byte = np.maximum(np.where(amax > 0, np.frexp(amax)[1] - 1 + 127, 0) - down, 1)
    scale = np.exp2(byte - 127.0)
    codes = (blocks / scale).astype(np.float32).astype(dtype).astype(np.float64)
    return np.moveaxis((codes * scale).reshape(v.shape), -1, axis)


WIDE = False


def mx_kscale(k):
    if not WIDE:
        return np.ones(k)
    levels = np.array([10, -10, 5, -5, 0])
    if k % 512:
        return np.exp2(np.random.permutation(np.resize(levels, k // 32))).repeat(32)
    a = np.empty((k // 512, 16))
    for p in range(k // 512):
        a[p, :8] = np.random.permutation(np.resize(levels, 8))
        for g in range(8):
            far = levels[np.abs(levels - a[p, g]) >= 10]
            a[p, g + 8] = far[np.random.randint(len(far))]
    return np.exp2(a.ravel()).repeat(32)


BF16 = ml_dtypes.bfloat16


def bf(x):
    return np.asarray(x, np.float32).astype(BF16)


def f64(x):
    return np.asarray(x).astype(np.float64)


M, G, P, L, H = 1024, 2048, 1024, 256, 512


def silu(v):
    return v / (1.0 + np.exp(-v))


def draw0():
    s = mx_kscale(G)
    t = mx_kscale(P)
    return {"x": bf(np.random.standard_normal((M, G)) * s),
            "w": bf(np.random.standard_normal((G, P)) / np.sqrt(G) / s[:, None]),
            "e": bf(np.random.standard_normal((G, H)) * s[:, None]),
            "cell_factor": bf(np.exp(0.3 * np.random.standard_normal(M))),
            "pathway_bias": bf(0.4 * np.random.standard_normal(P)),
            "activity_gain": bf((1.0 + 0.1 * np.random.standard_normal(P)) * t),
            "loading_gain": bf((1.0 + 0.1 * np.random.standard_normal(P)) / np.sqrt(P) / t),
            "latent_bias": bf(0.3 * np.random.standard_normal(H)),
            "noise": bf(np.random.standard_normal((M, L)))}


def core(x, w, e, cell_factor, pathway_bias, activity_gain, loading_gain, latent_bias, noise):
    wq = mxq(f64(w), 0, "e4m3")
    u = mxq(f64(x), 1, "e4m3") @ wq
    a = silu(f64(cell_factor)[:, None] * u + f64(pathway_bias)) * f64(activity_gain)
    v = wq.T @ mxq(f64(e), 0, "e4m3")
    v = v * f64(loading_gain)[:, None]
    q = (mxq(a, 1, "e4m3") @ mxq(v, 0, "e4m3")) + f64(latent_bias)
    mu = q[:, :L]
    sd = np.exp(0.5 * np.tanh(q[:, L:]))
    z = mu + sd * f64(noise)
    return mu, sd, z


def e4m3fn_bytes(y):
    return np.clip(np.asarray(y, np.float64), -448.0, 448.0).astype(np.float32).astype(ml_dtypes.float8_e4m3fn).view(np.uint8)


def e4m3fn_values(b):
    return np.asarray(b, np.uint8).view(ml_dtypes.float8_e4m3fn).astype(np.float64)


def setup_inputs():
    d = draw0()
    x0 = np.asarray(d['x']).astype(np.float64)
    s = (np.max(np.abs(x0), axis=(0,), keepdims=True) / 448.0).astype(np.float32)
    out = {}
    for k, v in d.items():
        if k == 'x':
            out['x_bytes'] = e4m3fn_bytes(x0 / s.astype(np.float64))
            out['x_scale'] = s
        else:
            out[k] = v
    return out


def reference(x_bytes, x_scale, w, e, cell_factor, pathway_bias, activity_gain, loading_gain, latent_bias, noise):
    return core(e4m3fn_values(x_bytes) * x_scale.astype(np.float64), w, e, cell_factor, pathway_bias, activity_gain, loading_gain, latent_bias, noise)

@@ -1,0 +1,497 @@
+from contextlib import ExitStack
+
+import concourse.mybir as mybir
+from concourse.masks import make_identity
+
+F32 = mybir.dt.float32
+BF16 = mybir.dt.bfloat16
+U32 = mybir.dt.uint32
+U8 = mybir.dt.uint8
+F8 = mybir.dt.float8_e4m3fn
+FP8X4 = mybir.dt.float8_e4m3fn_x4
+ACT = mybir.ActivationFunctionType
+ALU = mybir.AluOpType
+
+CELLS, GENES, PATHWAYS, LATENT = 1024, 2048, 1024, 256
+H = 2 * LATENT
+P = 128
+PASSES = GENES // 512
+GROUPS = PATHWAYS // 512
+HALVES = CELLS // 512
+FLOPS = 2 * CELLS * GENES * PATHWAYS + 2 * GENES * PATHWAYS * H + 2 * CELLS * PATHWAYS * H
+
+ORDER = [
+    ("P", 0, 0),
+    ("P", 0, 1),
+    ("P", 0, 2),
+    ("Tp", 0, 0),
+    ("P", 0, 3),
+    ("Ts", 0, 0),
+    ("P", 1, 1),
+    ("Tp", 0, 1),
+    ("Ts", 0, 1),
+    ("Ip", "w", 0, 0, 0),
+    ("P", 1, 0),
+    ("Ip", "w", 0, 0, 1),
+    ("Is", "w", 0, 0, 0),
+    ("Tp", 1, 1),
+    ("Is", "w", 0, 0, 1),
+    ("P", 2, 0),
+    ("Ip", "w", 1, 0, 0),
+    ("Ts", 1, 1),
+    ("Ip", "w", 1, 0, 1),
+    ("Is", "w", 1, 0, 0),
+    ("Tp", 1, 0),
+    ("Is", "w", 1, 0, 1),
+    ("Ip", "w", 2, 0, 0),
+    ("Ts", 1, 0),
+    ("WQ", "w", 0, 0),
+    ("Ip", "w", 2, 0, 1),
+    ("Is", "w", 2, 0, 0),
+    ("P", 3, 0),
+    ("Tp", 2, 0),
+    ("Is", "w", 2, 0, 1),
+    ("Ip", "w", 3, 0, 0),
+    ("Ts", 2, 0),
+    ("Ip", "w", 3, 0, 1),
+    ("Is", "w", 3, 0, 0),
+    ("Tp", 2, 1),
+    ("WQ", "w", 1, 0),
+    ("Is", "w", 3, 0, 1),
+    ("Tp", 3, 0),
+    ("P", 4, 0),
+    ("Ts", 2, 1),
+    ("Ip", "w", 1, 1, 1),
+    ("Ts", 3, 0),
+    ("Tp", 3, 1),
+    ("Is", "w", 1, 1, 1),
+    ("Ip", "w", 1, 1, 0),
+    ("Ts", 3, 1),
+    ("Ip", "w", 2, 1, 1),
+    ("P", 5, 0),
+    ("Is", "w", 1, 1, 0),
+    ("Tp", 4, 0),
+    ("Is", "w", 2, 1, 1),
+    ("Ip", "w", 3, 1, 0),
+    ("Ts", 4, 0),
+    ("Ip", "w", 3, 1, 1),
+    ("Is", "w", 3, 1, 0),
+    ("WQ", "w", 2, 0),
+    ("Tp", 4, 1),
+    ("Is", "w", 3, 1, 1),
+    ("WQ", "w", 3, 0),
+    ("Ip", "e", 0, 0, 0),
+    ("P", 6, 0),
+    ("Ip", "e", 0, 0, 1),
+    ("Is", "e", 0, 0, 0),
+    ("Tp", 5, 0),
+    ("Is", "e", 0, 0, 1),
+    ("Ip", "e", 1, 0, 0),
+    ("Ts", 5, 0),
+    ("Ip", "e", 1, 0, 1),
+    ("Is", "e", 1, 0, 0),
+    ("XQ", 0, 0),
+    ("Tp", 6, 0),
+    ("Is", "e", 1, 0, 1),
+    ("XQ", 0, 1),
+    ("Ip", "e", 2, 0, 0),
+    ("Ts", 6, 0),
+    ("XQ", 0, 2),
+    ("Ip", "e", 2, 0, 1),
+    ("Ts", 4, 1),
+    ("WQ", "e", 1, 0),
+    ("Tp", 6, 1),
+    ("XQ", 0, 3),
+    ("D", "e", 3, 0),
+    ("Tp", 5, 1),
+    ("P", 7, 0),
+    ("U", 0, 0, 3),
+    ("U", 0, 0, 0),
+    ("Ts", 6, 1),
+    ("WQ", "e", 0, 0),
+    ("U", 0, 0, 1),
+    ("Ts", 5, 1),
+    ("WQ", "e", 3, 0),
+    ("Is", "e", 2, 0, 0),
+    ("WQ", "w", 1, 1),
+    ("Tp", 7, 0),
+    ("Is", "e", 2, 0, 1),
+    ("WQ", "w", 3, 1),
+    ("Ip", "w", 0, 1, 0),
+    ("Ts", 7, 0),
+    ("WQ", "e", 2, 0),
+    ("Ip", "w", 0, 1, 1),
+    ("Is", "w", 0, 1, 0),
+    ("XQ", 1, 0),
+    ("VM", 0, 1),
+    ("Is", "w", 0, 1, 1),
+    ("XQ", 1, 1),
+    ("WQ", "w", 0, 1),
+    ("Tp", 7, 1),
+    ("VS", 0, 1),
+    ("C", 0, 0, 3),
+    ("Ip", "w", 2, 1, 0),
+    ("Ts", 7, 1),
+    ("C", 0, 0, 0),
+    ("VM", 0, 2),
+    ("SI", 0, 0, 3),
+    ("XQ", 1, 2),
+    ("SI", 0, 0, 0),
+    ("XQ", 1, 3),
+    ("VM", 0, 3),
+    ("VS", 0, 2),
+    ("C", 0, 0, 1),
+    ("Is", "w", 2, 1, 0),
+    ("VM", 0, 0),
+    ("VS", 0, 3),
+    ("WQ", "w", 2, 1),
+    ("SI", 0, 0, 1),
+    ("U", 0, 0, 2),
+    ("VS", 0, 0),
+    ("VI", 0),
+    ("U", 1, 0, 3),
+    ("C", 0, 0, 2),
+    ("U", 1, 0, 0),
+    ("C", 1, 0, 3),
+    ("U", 1, 0, 1),
+    ("C", 1, 0, 0),
+    ("SI", 0, 0, 2),
+    ("VQ", 0),
+    ("SI", 1, 0, 3),
+    ("U", 1, 0, 2),
+    ("C", 1, 0, 1),
+    ("SI", 1, 0, 0),
+    ("G", 0, 0),
+    ("SI", 1, 0, 1),
+    ("U", 1, 1, 0),
+    ("U", 1, 1, 1),
+    ("C", 1, 0, 2),
+    ("U", 1, 1, 2),
+    ("C", 1, 1, 0),
+    ("SI", 1, 0, 2),
+    ("C", 1, 1, 1),
+    ("SI", 1, 1, 0),
+    ("U", 1, 1, 3),
+    ("G", 1, 0),
+    ("SI", 1, 1, 1),
+    ("VM", 1, 0),
+    ("VM", 1, 1),
+    ("VS", 1, 0),
+    ("C", 1, 1, 2),
+    ("C", 1, 1, 3),
+    ("SI", 1, 1, 2),
+    ("VM", 1, 2),
+    ("AQ", 0, 0),
+    ("VS", 1, 1),
+    ("AQ", 1, 0),
+    ("SI", 1, 1, 3),
+    ("VM", 1, 3),
+    ("VS", 1, 2),
+    ("G", 1, 1),
+    ("U", 0, 1, 0),
+    ("VS", 1, 3),
+    ("VI", 1),
+    ("U", 0, 1, 1),
+    ("C", 0, 1, 0),
+    ("U", 0, 1, 2),
+    ("AQ", 1, 1),
+    ("C", 0, 1, 1),
+    ("SI", 0, 1, 0),
+    ("U", 0, 1, 3),
+    ("VQ", 1),
+    ("SI", 0, 1, 1),
+    ("C", 0, 1, 2),
+    ("Q", 0, 0),
+    ("C", 0, 1, 3),
+    ("Q", 0, 1),
+    ("SI", 0, 1, 2),
+    ("Q", 1, 0),
+    ("QB", 0),
+    ("Q", 2, 0),
+    ("SI", 0, 1, 3),
+    ("Q", 3, 0),
+    ("Q", 1, 1),
+    ("TH", 0),
+    ("Q", 2, 1),
+    ("G", 0, 1),
+    ("Q", 3, 1),
+    ("QB", 3),
+    ("AQ", 0, 1),
+    ("TH", 3),
+    ("QB", 1),
+    ("Q", 4, 0),
+    ("Q", 5, 0),
+    ("QB", 2),
+    ("Q", 5, 1),
+    ("TH", 1),
+    ("Q", 6, 0),
+    ("QB", 5),
+    ("Q", 7, 0),
+    ("TH", 2),
+    ("Q", 4, 1),
+    ("Z", 0),
+    ("Q", 6, 1),
+    ("TH", 5),
+    ("Q", 7, 1),
+    ("QB", 6),
+    ("QB", 7),
+    ("TH", 6),
+    ("QB", 4),
+    ("TH", 7),
+    ("Z", 3),
+    ("TH", 4),
+    ("Z", 1),
+    ("Z", 2),
+    ("Z", 5),
+    ("Z", 6),
+    ("Z", 7),
+    ("Z", 4),
+]
+
+
+def tile_pathway_latent_encoder_f5_kernel(
+    tc, x_bytes, x_scale, w, e, cell_factor, pathway_bias, activity_gain, loading_gain, latent_bias, noise, mu_out, sd_out, z_out
+):
+    nc = tc.nc
+    with ExitStack() as ctx:
+        keep = ctx.enter_context(tc.tile_pool(name="keep", bufs=1))
+        xin = ctx.enter_context(tc.tile_pool(name="xin", bufs=4))
+        work = ctx.enter_context(tc.tile_pool(name="work", bufs=2))
+        xgp = ctx.enter_context(tc.tile_pool(name="xgp", bufs=3))
+        grp = ctx.enter_context(tc.tile_pool(name="grp", bufs=5))
+        outs = ctx.enter_context(tc.tile_pool(name="outs", bufs=5))
+        qbp = ctx.enter_context(tc.tile_pool(name="qbp", bufs=8))
+        rawp = ctx.enter_context(tc.tile_pool(name="rawp", bufs=10))
+        ps_tr = ctx.enter_context(tc.psum_pool(name="ps_tr", bufs=2))
+        ps_id = ctx.enter_context(tc.psum_pool(name="ps_id", bufs=2))
+        ps_mx = ctx.enter_context(tc.psum_pool(name="ps_mx", bufs=4))
+        ctx.enter_context(tc.manual_schedule())
+
+        scale_row = x_scale.rearrange("o k -> (o k)")
+        scale_b = keep.tile([P, GENES], F32, name="scale_b")
+        x_raw = {}
+        w_raw = {}
+        e_raw = {}
+
+        def load(what):
+            kind = what[0]
+            if kind == "s":
+                c = int(what[1])
+                nc.sync.dma_start(out=scale_b[:, c * 512 : (c + 1) * 512], in_=scale_row[c * 512 : (c + 1) * 512].partition_broadcast(P))
+            elif kind == "x":
+                i = int(what[1])
+                x_raw[i] = xin.tile([P, GENES], U8, name="x_raw")
+                nc.sync.dma_start(out=x_raw[i][:], in_=x_bytes[i * P : (i + 1) * P, :])
+            elif kind == "w":
+                g, jg = int(what[1]), int(what[2])
+                w_raw[g, jg] = rawp.tile([P, 4, 512], BF16, name="raw")
+                nc.sync.dma_start(
+                    out=w_raw[g, jg][:], in_=w[g * 512 : (g + 1) * 512, jg * 512 : (jg + 1) * 512].rearrange("(p j) n -> p j n", j=4)
+                )
+            elif kind == "e":
+                g = int(what[1])
+                e_raw[g] = rawp.tile([P, 4, H], BF16, name="raw")
+                nc.sync.dma_start(out=e_raw[g][:], in_=e[g * 512 : (g + 1) * 512, :].rearrange("(p j) n -> p j n", j=4))
+
+        warm = keep.tile([P, 1], F32, name="warm")
+        nc.gpsimd.memset(warm[:], 0.0)
+        ident = keep.tile([P, P], F32, name="ident")
+        make_identity(nc, ident[:])
+        ident_bf = keep.tile([P, P], BF16, name="ident_bf")
+        make_identity(nc, ident_bf[:])
+        nc.scalar.activation(out=warm[:], in_=warm[:], func=ACT.Silu)
+        for what in ("s0", "x0", "s1", "s2", "s3", "x1", "w00", "w10", "x2", "w20", "w30", "x3", "w01"):
+            load(what)
+
+        cf_b = keep.tile([P, CELLS], BF16, name="cf_b")
+        lb_b = keep.tile([P, H], BF16, name="lb_b")
+        pb_t = keep.tile([P, GROUPS, 4], BF16, name="pb_t")
+        ag_t = keep.tile([P, GROUPS, 4], BF16, name="ag_t")
+        lg_t = keep.tile([P, GROUPS, 4], BF16, name="lg_t")
+        lg_f = keep.tile([P, GROUPS, 4], F32, name="lg_f")
+        noise_t = keep.tile([P, CELLS // P, LATENT], BF16, name="noise_t")
+        nc.gpsimd.dma_start(out=pb_t[:], in_=pathway_bias.rearrange("(g p t) -> p g t", p=P, t=4))
+        nc.gpsimd.dma_start(out=ag_t[:], in_=activity_gain.rearrange("(g p t) -> p g t", p=P, t=4))
+        nc.gpsimd.dma_start(out=lg_t[:], in_=loading_gain.rearrange("(g p t) -> p g t", p=P, t=4))
+        nc.gpsimd.tensor_copy(out=lg_f[:], in_=lg_t[:])
+
+        LATER = {0: ("x4", "w11"), 1: ("x5", "w21"), 2: ("x6", "w31"), 3: ("x7", "e0", "e1", "e2", "e3", "cf", "lb", "noise")}
+
+        xc = [keep.tile([P, PASSES, 512], U32, name=f"xc{h}", align_bytes=64) for h in range(HALVES)]
+        xs = [keep.tile([P, PASSES, 512], U8, name=f"xs{h}", align_bytes=64) for h in range(HALVES)]
+        wc = {}
+        ws = {}
+        for g in range(PASSES):
+            for jg in range(GROUPS):
+                wc["w", g, jg] = keep.tile([P, 512], U32, name=f"wc{g}{jg}", align_bytes=64)
+                ws["w", g, jg] = keep.tile([P, 512], U8, name=f"ws{g}{jg}", align_bytes=64)
+            wc["e", g, 0] = keep.tile([P, H], U32, name=f"ec{g}", align_bytes=64)
+            ws["e", g, 0] = keep.tile([P, H], U8, name=f"es{g}", align_bytes=64)
+        ac = [[keep.tile([P, 512], U32, name=f"ac{jg}{h}", align_bytes=64) for h in range(HALVES)] for jg in range(GROUPS)]
+        asc = [[keep.tile([P, 512], U8, name=f"asc{jg}{h}", align_bytes=64) for h in range(HALVES)] for jg in range(GROUPS)]
+        vc = [keep.tile([P, H], U32, name=f"vc{jg}", align_bytes=64) for jg in range(GROUPS)]
+        vsc = [keep.tile([P, H], U8, name=f"vsc{jg}", align_bytes=64) for jg in range(GROUPS)]
+        vl = [keep.tile([P, 4, 512], BF16, name=f"vl{jg}") for jg in range(GROUPS)]
+
+        T = {}
+
+        def get(pool, tag, key, shape, dt, **kw):
+            if key not in T:
+                T[key] = pool.tile(shape, dt, name=tag, **kw)
+            return T[key]
+
+        def P_(i, c):
+            n = {0: 4, 1: 2}.get(i, 1)
+            xw = get(work, "xw", ("xw", i), [P, GENES], BF16, align_bytes=64)
+            s = slice(c * GENES // n, (c + 1) * GENES // n)
+            nc.vector.tensor_tensor(out=xw[:, s], in0=x_raw[i][:, s].bitcast(F8), in1=scale_b[:, s], op=ALU.mult)
+            if c == n - 1 and i in LATER:
+                for what in LATER[i]:
+                    if what == "cf":
+                        nc.sync.dma_start(out=cf_b[:], in_=cell_factor.partition_broadcast(P))
+                    elif what == "lb":
+                        nc.sync.dma_start(out=lb_b[:], in_=latent_bias.partition_broadcast(P))
+                    elif what == "noise":
+                        nc.sync.dma_start(out=noise_t[:], in_=noise.rearrange("(t p) l -> p t l", p=P))
+                    else:
+                        load(what)
+
+        def Tp(i, gp):
+            bank = get(ps_tr, "tr", ("tr", i, gp), [P, 2, 2, P], F32)
+            words = T["xw", i][:].bitcast(F32)
+            for gi in range(2):
+                g = 2 * gp + gi
+                for u in range(2):
+                    nc.tensor.transpose(bank[:, gi, u, :], words[:, 256 * g + u : 256 * (g + 1) : 2], ident[:])
+
+        def Ts(i, gp):
+            h, mt = divmod(i, 4)
+            xg = get(xgp, "xg", ("xg", h, gp), [P, 2, 512, 4], BF16, align_bytes=64)
+            dst = xg[:].rearrange("p g m t -> p (g m t)").bitcast(F32).rearrange("p (g m u) -> p g m u", g=2, u=2)
+            nc.scalar.copy(out=dst[:, :, mt * P : (mt + 1) * P, :], in_=T["tr", i, gp][:].rearrange("p g u m -> p g m u"))
+
+        def XQ(h, g):
+            src = T["xg", h, g // 2][:, g % 2, :, :].rearrange("p m t -> p (m t)")
+            nc.vector.quantize_mx(out=xc[h][:, g, :].bitcast(FP8X4), scales=xs[h][:, g, :], in_=src)
+
+        def raw(u):
+            if u[0] == "w":
+                return w_raw[u[1], u[2]][:].rearrange("p j (m t) -> p j t m", t=4)
+            return e_raw[u[1]][:].rearrange("p j (t m) -> p j t m", t=4)
+
+        def Ip(k, g, jg, b):
+            u = (k, g, jg)
+            bank = get(ps_id, "idb", ("id", u, b), [P, 1024], BF16)
+            for i in range(2):
+                nc.tensor.matmul(
+                    bank[:, i * 512 : (i + 1) * 512],
+                    lhsT=ident_bf[:],
+                    rhs=raw(u)[:, :, 2 * b + i, :].rearrange("p j m -> p m j"),
+                    start=True,
+                    stop=True,
+                )
+
+        def Is(k, g, jg, b):
+            u = (k, g, jg)
+            dst = get(grp, "gr", ("gr", u), [P, 2048], BF16, align_bytes=64)
+            nc.scalar.copy(out=dst[:, b * 1024 : (b + 1) * 1024], in_=T["id", u, b][:])
+
+        def D(k, g, jg):
+            dst = get(grp, "gr", ("gr", (k, g, jg)), [P, 2048], BF16, align_bytes=64)
+            if k == "w":
+                nc.scalar.copy(out=dst[:].rearrange("p (t m j) -> p t m j", t=4, j=4), in_=raw((k, g, jg)).rearrange("p j t m -> p t m j"))
+            else:
+                nc.scalar.copy(
+                    out=dst[:].rearrange("p (c i j) -> p c j i", i=4, j=4), in_=e_raw[g][:].rearrange("p j (c i) -> p c j i", i=4)
+                )
+
+        def WQ(k, g, jg):
+            u = (k, g, jg)
+            nc.vector.quantize_mx(out=wc[u][:].bitcast(FP8X4), scales=ws[u][:], in_=T["gr", u][:])
+
+        def mx(bank, t, jg, rhs, rhs_s):
+            col = slice(t * P, (t + 1) * P)
+            for g in range(PASSES):
+                nc.tensor.matmul_mx(
+                    out=bank[:],
+                    lhsT=wc["w", g, jg][:, col].bitcast(FP8X4),
+                    lhsT_scale=ws["w", g, jg][:, col],
+                    rhs=rhs(g).bitcast(FP8X4),
+                    rhs_scale=rhs_s(g),
+                    start=(g == 0),
+                    stop=(g == PASSES - 1),
+                )
+
+        def U(jg, h, t):
+            bank = get(ps_mx, "mx", ("u", jg, h, t), [P, 512], F32)
+            mx(bank, t, jg, lambda g: xc[h][:, g, :], lambda g: xs[h][:, g, :])
+
+        def C(jg, h, t):
+            y = get(work, "y", ("y", jg, h), [P, 4, 512], F32)
+            nc.vector.tensor_tensor(out=y[:, t, :], in0=T["u", jg, h, t][:], in1=cf_b[:, h * 512 : (h + 1) * 512], op=ALU.mult)
+
+        def SI(jg, h, t):
+            y = T["y", jg, h]
+            nc.scalar.activation(out=y[:, t, :], in_=y[:, t, :], func=ACT.Silu, bias=pb_t[:, jg, t : t + 1])
+
+        def G(jg, h):
+            dst = get(grp, "gr", ("gr", ("a", jg, h)), [P, 2048], BF16, align_bytes=64)
+            nc.vector.tensor_tensor(
+                out=dst[:].rearrange("p (m t) -> p m t", t=4),
+                in0=T["y", jg, h][:].rearrange("p t m -> p m t"),
+                in1=ag_t[:, jg, :].unsqueeze(1).to_broadcast([P, 512, 4]),
+                op=ALU.mult,
+            )
+
+        def AQ(jg, h):
+            nc.vector.quantize_mx(out=ac[jg][h][:].bitcast(FP8X4), scales=asc[jg][h][:], in_=T["gr", ("a", jg, h)][:])
+
+        def VM(jg, t):
+            bank = get(ps_mx, "mx", ("v", jg, t), [P, 512], F32)
+            mx(bank, t, jg, lambda g: wc["e", g, 0][:], lambda g: ws["e", g, 0][:])
+
+        def VS(jg, t):
+            nc.scalar.activation(out=vl[jg][:, t, :], in_=T["v", jg, t][:], func=ACT.Copy, scale=lg_f[:, jg, t : t + 1])
+
+        def VI(jg):
+            dst = get(grp, "gr", ("gr", ("v", jg)), [P, 2048], BF16, align_bytes=64)
+            nc.scalar.copy(out=dst[:].rearrange("p (c i t) -> p c t i", i=4, t=4), in_=vl[jg][:].rearrange("p t (c i) -> p c t i", i=4))
+
+        def VQ(jg):
+            nc.vector.quantize_mx(out=vc[jg][:].bitcast(FP8X4), scales=vsc[jg][:], in_=T["gr", ("v", jg)][:])
+
+        def Q(mt, jg):
+            h, m = divmod(mt, 4)
+            rows = slice(m * P, (m + 1) * P)
+            bank = get(ps_mx, "mx", ("q", mt), [P, 512], F32)
+            nc.tensor.matmul_mx(
+                out=bank[:],
+                lhsT=ac[jg][h][:, rows].bitcast(FP8X4),
+                lhsT_scale=asc[jg][h][:, rows],
+                rhs=vc[jg][:].bitcast(FP8X4),
+                rhs_scale=vsc[jg][:],
+                start=(jg == 0),
+                stop=(jg == 1),
+            )
+
+        def QB(mt):
+            qb = get(qbp, "qb", ("qb", mt), [P, H], F32)
+            nc.vector.tensor_tensor(out=qb[:], in0=T["q", mt][:], in1=lb_b[:], op=ALU.add)
+            nc.sync.dma_start(out=mu_out[mt * P : (mt + 1) * P, :], in_=qb[:, 0:LATENT])
+
+        def TH(mt):
+            qb = T["qb", mt]
+            sd = get(outs, "sd", ("sd", mt), [P, LATENT], F32)
+            nc.scalar.activation(out=sd[:], in_=qb[:, LATENT:H], func=ACT.Tanh)
+            nc.scalar.activation(out=sd[:], in_=sd[:], func=ACT.Exp, scale=0.5)
+            nc.sync.dma_start(out=sd_out[mt * P : (mt + 1) * P, :], in_=sd[:])
+
+        def Z(mt):
+            z = get(outs, "z", ("z", mt), [P, LATENT], F32)
+            nc.vector.tensor_tensor(out=z[:], in0=T["sd", mt][:], in1=noise_t[:, mt, :], op=ALU.mult)
+            nc.vector.tensor_tensor(out=z[:], in0=z[:], in1=T["qb", mt][:, 0:LATENT], op=ALU.add)
+            nc.sync.dma_start(out=z_out[mt * P : (mt + 1) * P, :], in_=z[:])
+
+        steps = dict(P=P_, Tp=Tp, Ts=Ts, XQ=XQ, Ip=Ip, Is=Is, D=D, WQ=WQ, U=U, C=C, SI=SI, G=G, AQ=AQ, VM=VM, VS=VS, VI=VI, VQ=VQ, Q=Q, QB=QB, TH=TH, Z=Z)
+        for step in ORDER:
+            steps[step[0]](*step[1:])

@@ -18,234 +18,187 @@ P = 128
 PASSES = GENES // 512
 GROUPS = PATHWAYS // 512
 HALVES = CELLS // 512
+TILES = CELLS // P
+TR = 2
+ON_VECTOR = {("w", 0, 0)}
+FIRST_LOADS = ("x0", "w00", "w10", "x1", "w20", "w30", "x2",)
+LOADS_AFTER = {1: ("w01", "w11", "x3", "w21", "w31",), 5: ("e0", "e1", "e2", "e3", "noise",)}
 FLOPS = 2 * CELLS * GENES * PATHWAYS + 2 * GENES * PATHWAYS * H + 2 * CELLS * PATHWAYS * H
 
 ORDER = [
-    ("P", 0, 0),
-    ("P", 0, 1),
-    ("P", 0, 2),
+    ("K", 0),
+    ("K", 1),
+    ("D", "w", 0, 0),
+    ("CF", 0),
     ("Tp", 0, 0),
-    ("P", 0, 3),
-    ("Ts", 0, 0),
-    ("P", 1, 1),
-    ("Tp", 0, 1),
-    ("Ts", 0, 1),
-    ("Ip", "w", 0, 0, 0),
-    ("P", 1, 0),
-    ("Ip", "w", 0, 0, 1),
-    ("Is", "w", 0, 0, 0),
-    ("Tp", 1, 1),
-    ("Is", "w", 0, 0, 1),
-    ("P", 2, 0),
-    ("Ip", "w", 1, 0, 0),
-    ("Ts", 1, 1),
-    ("Ip", "w", 1, 0, 1),
-    ("Is", "w", 1, 0, 0),
-    ("Tp", 1, 0),
-    ("Is", "w", 1, 0, 1),
-    ("Ip", "w", 2, 0, 0),
-    ("Ts", 1, 0),
     ("WQ", "w", 0, 0),
-    ("Ip", "w", 2, 0, 1),
-    ("Is", "w", 2, 0, 0),
-    ("P", 3, 0),
-    ("Tp", 2, 0),
-    ("Is", "w", 2, 0, 1),
-    ("Ip", "w", 3, 0, 0),
-    ("Ts", 2, 0),
-    ("Ip", "w", 3, 0, 1),
-    ("Is", "w", 3, 0, 0),
-    ("Tp", 2, 1),
-    ("WQ", "w", 1, 0),
-    ("Is", "w", 3, 0, 1),
-    ("Tp", 3, 0),
-    ("P", 4, 0),
-    ("Ts", 2, 1),
-    ("Ip", "w", 1, 1, 1),
-    ("Ts", 3, 0),
-    ("Tp", 3, 1),
-    ("Is", "w", 1, 1, 1),
-    ("Ip", "w", 1, 1, 0),
-    ("Ts", 3, 1),
-    ("Ip", "w", 2, 1, 1),
-    ("P", 5, 0),
-    ("Is", "w", 1, 1, 0),
-    ("Tp", 4, 0),
-    ("Is", "w", 2, 1, 1),
-    ("Ip", "w", 3, 1, 0),
-    ("Ts", 4, 0),
-    ("Ip", "w", 3, 1, 1),
-    ("Is", "w", 3, 1, 0),
-    ("WQ", "w", 2, 0),
-    ("Tp", 4, 1),
-    ("Is", "w", 3, 1, 1),
-    ("WQ", "w", 3, 0),
-    ("Ip", "e", 0, 0, 0),
-    ("P", 6, 0),
-    ("Ip", "e", 0, 0, 1),
-    ("Is", "e", 0, 0, 0),
-    ("Tp", 5, 0),
-    ("Is", "e", 0, 0, 1),
-    ("Ip", "e", 1, 0, 0),
-    ("Ts", 5, 0),
-    ("Ip", "e", 1, 0, 1),
-    ("Is", "e", 1, 0, 0),
+    ("Tp", 0, 1),
+    ("PP", 0, 0),
+    ("K", 2),
+    ("PP", 0, 1),
+    ("Tp", 0, 2),
+    ("K", 3),
+    ("PP", 0, 2),
+    ("Tp", 0, 3),
+    ("D", "w", 1, 0),
     ("XQ", 0, 0),
-    ("Tp", 6, 0),
-    ("Is", "e", 1, 0, 1),
+    ("Tp", 1, 0),
+    ("PP", 0, 3),
+    ("PP", 1, 0),
+    ("Tp", 1, 3),
+    ("K", 4),
     ("XQ", 0, 1),
-    ("Ip", "e", 2, 0, 0),
-    ("Ts", 6, 0),
-    ("XQ", 0, 2),
-    ("Ip", "e", 2, 0, 1),
-    ("Ts", 4, 1),
-    ("WQ", "e", 1, 0),
-    ("Tp", 6, 1),
-    ("XQ", 0, 3),
-    ("D", "e", 3, 0),
-    ("Tp", 5, 1),
-    ("P", 7, 0),
-    ("U", 0, 0, 3),
-    ("U", 0, 0, 0),
-    ("Ts", 6, 1),
-    ("WQ", "e", 0, 0),
-    ("U", 0, 0, 1),
-    ("Ts", 5, 1),
-    ("WQ", "e", 3, 0),
-    ("Is", "e", 2, 0, 0),
-    ("WQ", "w", 1, 1),
-    ("Tp", 7, 0),
-    ("Is", "e", 2, 0, 1),
-    ("WQ", "w", 3, 1),
-    ("Ip", "w", 0, 1, 0),
-    ("Ts", 7, 0),
-    ("WQ", "e", 2, 0),
-    ("Ip", "w", 0, 1, 1),
-    ("Is", "w", 0, 1, 0),
-    ("XQ", 1, 0),
-    ("VM", 0, 1),
-    ("Is", "w", 0, 1, 1),
+    ("Tp", 1, 2),
+    ("K", 5),
+    ("WQ", "w", 1, 0),
+    ("PP", 1, 3),
+    ("D", "w", 2, 0),
+    ("PP", 1, 2),
+    ("Tp", 2, 0),
+    ("PP", 2, 0),
+    ("Tp", 2, 2),
+    ("D", "w", 3, 0),
     ("XQ", 1, 1),
+    ("Tp", 2, 3),
+    ("WQ", "w", 2, 0),
+    ("PP", 2, 2),
+    ("D", "w", 0, 1),
+    ("PP", 2, 3),
+    ("Tp", 1, 1),
+    ("WQ", "w", 3, 0),
+    ("Tp", 2, 1),
+    ("PP", 1, 1),
+    ("K", 6),
     ("WQ", "w", 0, 1),
-    ("Tp", 7, 1),
-    ("VS", 0, 1),
-    ("C", 0, 0, 3),
-    ("Ip", "w", 2, 1, 0),
-    ("Ts", 7, 1),
+    ("XQ", 1, 0),
+    ("K", 7),
+    ("XQ", 2, 1),
+    ("U", 0, ("h", 0), 0),
+    ("PP", 2, 1),
+    ("D", "w", 1, 1),
+    ("Tp", 3, 2),
     ("C", 0, 0, 0),
-    ("VM", 0, 2),
-    ("SI", 0, 0, 3),
-    ("XQ", 1, 2),
+    ("Tp", 3, 0),
+    ("XQ", 2, 0),
+    ("U", 0, ("h", 0), 1),
+    ("PP", 3, 2),
     ("SI", 0, 0, 0),
-    ("XQ", 1, 3),
-    ("VM", 0, 3),
-    ("VS", 0, 2),
-    ("C", 0, 0, 1),
-    ("Is", "w", 2, 1, 0),
-    ("VM", 0, 0),
-    ("VS", 0, 3),
+    ("U", 0, ("h", 0), 2),
+    ("D", "w", 2, 1),
+    ("WQ", "w", 1, 1),
+    ("PP", 3, 0),
+    ("Tp", 3, 1),
+    ("U", 0, ("h", 0), 3),
+    ("PP", 3, 1),
+    ("D", "w", 3, 1),
+    ("Tp", 3, 3),
     ("WQ", "w", 2, 1),
-    ("SI", 0, 0, 1),
-    ("U", 0, 0, 2),
-    ("VS", 0, 0),
-    ("VI", 0),
-    ("U", 1, 0, 3),
+    ("XQ", 3, 0),
+    ("PP", 3, 3),
+    ("D", "e", 0, 0),
+    ("C", 0, 0, 1),
+    ("WQ", "w", 3, 1),
+    ("XQ", 3, 1),
+    ("U", 1, ("h", 0), 0),
     ("C", 0, 0, 2),
-    ("U", 1, 0, 0),
-    ("C", 1, 0, 3),
-    ("U", 1, 0, 1),
-    ("C", 1, 0, 0),
+    ("C", 0, 0, 3),
+    ("SI", 0, 0, 1),
+    ("U", 1, ("h", 0), 1),
+    ("WQ", "e", 0, 0),
     ("SI", 0, 0, 2),
-    ("VQ", 0),
-    ("SI", 1, 0, 3),
-    ("U", 1, 0, 2),
+    ("C", 1, 0, 0),
+    ("U", 1, ("h", 0), 2),
+    ("SI", 0, 0, 3),
     ("C", 1, 0, 1),
     ("SI", 1, 0, 0),
     ("G", 0, 0),
+    ("U", 1, ("h", 0), 3),
     ("SI", 1, 0, 1),
-    ("U", 1, 1, 0),
-    ("U", 1, 1, 1),
+    ("D", "e", 1, 0),
+    ("U", 0, ("h", 1), 0),
     ("C", 1, 0, 2),
-    ("U", 1, 1, 2),
-    ("C", 1, 1, 0),
+    ("U", 0, ("h", 1), 1),
+    ("C", 1, 0, 3),
     ("SI", 1, 0, 2),
-    ("C", 1, 1, 1),
-    ("SI", 1, 1, 0),
-    ("U", 1, 1, 3),
+    ("C", 0, 1, 0),
+    ("U", 0, ("h", 1), 2),
+    ("WQ", "e", 1, 0),
+    ("SI", 1, 0, 3),
+    ("U", 0, ("h", 1), 3),
+    ("AQ", 0, 0),
+    ("SI", 0, 1, 0),
+    ("D", "e", 2, 0),
     ("G", 1, 0),
+    ("U", 1, ("h", 1), 0),
+    ("U", 1, ("h", 1), 1),
+    ("C", 0, 1, 2),
+    ("D", "e", 3, 0),
+    ("U", 1, ("h", 1), 2),
+    ("WQ", "e", 2, 0),
+    ("C", 0, 1, 3),
+    ("U", 1, ("h", 1), 3),
+    ("C", 1, 1, 0),
+    ("C", 1, 1, 1),
+    ("C", 1, 1, 2),
+    ("SI", 0, 1, 3),
+    ("WQ", "e", 3, 0),
+    ("SI", 1, 1, 0),
+    ("C", 1, 1, 3),
     ("SI", 1, 1, 1),
+    ("VM", 0, 3),
+    ("AQ", 1, 0),
+    ("SI", 1, 1, 2),
+    ("C", 0, 1, 1),
+    ("VM", 0, 0),
+    ("SI", 1, 1, 3),
+    ("VS", 0, 3),
+    ("G", 1, 1),
+    ("VM", 0, 1),
+    ("SI", 0, 1, 1),
+    ("SI", 0, 1, 2),
+    ("VM", 0, 2),
+    ("VS", 0, 1),
+    ("G", 0, 1),
+    ("VS", 0, 0),
     ("VM", 1, 0),
+    ("VS", 0, 2),
     ("VM", 1, 1),
     ("VS", 1, 0),
-    ("C", 1, 1, 2),
-    ("C", 1, 1, 3),
-    ("SI", 1, 1, 2),
+    ("VI", 0),
     ("VM", 1, 2),
-    ("AQ", 0, 0),
     ("VS", 1, 1),
-    ("AQ", 1, 0),
-    ("SI", 1, 1, 3),
+    ("AQ", 1, 1),
     ("VM", 1, 3),
     ("VS", 1, 2),
-    ("G", 1, 1),
-    ("U", 0, 1, 0),
+    ("VQ", 0),
+    ("AQ", 0, 1),
     ("VS", 1, 3),
     ("VI", 1),
-    ("U", 0, 1, 1),
-    ("C", 0, 1, 0),
-    ("U", 0, 1, 2),
-    ("AQ", 1, 1),
-    ("C", 0, 1, 1),
-    ("SI", 0, 1, 0),
-    ("U", 0, 1, 3),
     ("VQ", 1),
-    ("SI", 0, 1, 1),
-    ("C", 0, 1, 2),
-    ("Q", 0, 0),
-    ("C", 0, 1, 3),
-    ("Q", 0, 1),
-    ("SI", 0, 1, 2),
-    ("Q", 1, 0),
+    ("Q", 0),
+    ("Q", 1),
     ("QB", 0),
-    ("Q", 2, 0),
-    ("SI", 0, 1, 3),
-    ("Q", 3, 0),
-    ("Q", 1, 1),
-    ("TH", 0),
-    ("Q", 2, 1),
-    ("G", 0, 1),
-    ("Q", 3, 1),
-    ("QB", 3),
-    ("AQ", 0, 1),
-    ("TH", 3),
+    ("Q", 2),
     ("QB", 1),
-    ("Q", 4, 0),
-    ("Q", 5, 0),
+    ("Q", 3),
     ("QB", 2),
-    ("Q", 5, 1),
-    ("TH", 1),
-    ("Q", 6, 0),
+    ("TH", 0),
+    ("Q", 4),
+    ("QB", 3),
+    ("Q", 5),
+    ("QB", 4),
+    ("Q", 6),
     ("QB", 5),
-    ("Q", 7, 0),
-    ("TH", 2),
-    ("Q", 4, 1),
-    ("Z", 0),
-    ("Q", 6, 1),
-    ("TH", 5),
-    ("Q", 7, 1),
+    ("Q", 7),
     ("QB", 6),
     ("QB", 7),
-    ("TH", 6),
-    ("QB", 4),
-    ("TH", 7),
-    ("Z", 3),
-    ("TH", 4),
+    ("TH", 1),
+    ("Z", 0),
+    ("TH", 3),
     ("Z", 1),
+    ("TH", 2),
+    ("Z", 3),
     ("Z", 2),
-    ("Z", 5),
-    ("Z", 6),
-    ("Z", 7),
-    ("Z", 4),
 ]
 
 
@@ -255,70 +208,71 @@ def tile_pathway_latent_encoder_f5_kernel(
     nc = tc.nc
     with ExitStack() as ctx:
         keep = ctx.enter_context(tc.tile_pool(name="keep", bufs=1))
-        xin = ctx.enter_context(tc.tile_pool(name="xin", bufs=4))
-        work = ctx.enter_context(tc.tile_pool(name="work", bufs=2))
-        xgp = ctx.enter_context(tc.tile_pool(name="xgp", bufs=3))
+        xin = ctx.enter_context(tc.tile_pool(name="xin", bufs=3))
+        xwp = ctx.enter_context(tc.tile_pool(name="xwp", bufs=2))
+        xgp = ctx.enter_context(tc.tile_pool(name="xgp", bufs=2))
+        yp = ctx.enter_context(tc.tile_pool(name="yp", bufs=2))
         grp = ctx.enter_context(tc.tile_pool(name="grp", bufs=5))
-        outs = ctx.enter_context(tc.tile_pool(name="outs", bufs=5))
-        qbp = ctx.enter_context(tc.tile_pool(name="qbp", bufs=8))
+        outs = ctx.enter_context(tc.tile_pool(name="outs", bufs=3))
+        qbp = ctx.enter_context(tc.tile_pool(name="qbp", bufs=4))
         rawp = ctx.enter_context(tc.tile_pool(name="rawp", bufs=10))
-        ps_tr = ctx.enter_context(tc.psum_pool(name="ps_tr", bufs=2))
-        ps_id = ctx.enter_context(tc.psum_pool(name="ps_id", bufs=2))
-        ps_mx = ctx.enter_context(tc.psum_pool(name="ps_mx", bufs=4))
+        ps_tr = ctx.enter_context(tc.psum_pool(name="ps_tr", bufs=TR))
+        ps_mx = ctx.enter_context(tc.psum_pool(name="ps_mx", bufs=8 - TR))
         ctx.enter_context(tc.manual_schedule())
 
-        scale_row = x_scale.rearrange("o k -> (o k)")
-        scale_b = keep.tile([P, GENES], F32, name="scale_b")
         x_raw = {}
-        w_raw = {}
-        e_raw = {}
+        raws = {}
+        x_rows = x_bytes.rearrange("(p i) k -> p i k", i=TILES)
 
         def load(what):
             kind = what[0]
-            if kind == "s":
-                c = int(what[1])
-                nc.sync.dma_start(out=scale_b[:, c * 512 : (c + 1) * 512], in_=scale_row[c * 512 : (c + 1) * 512].partition_broadcast(P))
-            elif kind == "x":
-                i = int(what[1])
-                x_raw[i] = xin.tile([P, GENES], U8, name="x_raw")
-                nc.sync.dma_start(out=x_raw[i][:], in_=x_bytes[i * P : (i + 1) * P, :])
+            if kind == "x":
+                pr = int(what[1])
+                x_raw[pr] = xin.tile([P, 2, GENES], U8, name="x_raw")
+                nc.sync.dma_start(out=x_raw[pr][:], in_=x_rows[:, 2 * pr : 2 * pr + 2, :])
             elif kind == "w":
                 g, jg = int(what[1]), int(what[2])
-                w_raw[g, jg] = rawp.tile([P, 4, 512], BF16, name="raw")
+                raws["w", g, jg] = rawp.tile([P, 4, 512], BF16, name="raw")
                 nc.sync.dma_start(
-                    out=w_raw[g, jg][:], in_=w[g * 512 : (g + 1) * 512, jg * 512 : (jg + 1) * 512].rearrange("(p j) n -> p j n", j=4)
+                    out=raws["w", g, jg][:], in_=w[g * 512 : (g + 1) * 512, jg * 512 : (jg + 1) * 512].rearrange("(p j) n -> p j n", j=4)
                 )
             elif kind == "e":
                 g = int(what[1])
-                e_raw[g] = rawp.tile([P, 4, H], BF16, name="raw")
-                nc.sync.dma_start(out=e_raw[g][:], in_=e[g * 512 : (g + 1) * 512, :].rearrange("(p j) n -> p j n", j=4))
+                raws["e", g, 0] = rawp.tile([P, 4, H], BF16, name="raw")
+                nc.sync.dma_start(out=raws["e", g, 0][:], in_=e[g * 512 : (g + 1) * 512, :].rearrange("(p j) n -> p j n", j=4))
+            else:
+                nc.sync.dma_start(out=noise_t[:], in_=noise.rearrange("(p i) l -> p i l", i=TILES))
 
         warm = keep.tile([P, 1], F32, name="warm")
         nc.gpsimd.memset(warm[:], 0.0)
-        ident = keep.tile([P, P], F32, name="ident")
-        make_identity(nc, ident[:])
         ident_bf = keep.tile([P, P], BF16, name="ident_bf")
         make_identity(nc, ident_bf[:])
-        nc.scalar.activation(out=warm[:], in_=warm[:], func=ACT.Silu)
-        for what in ("s0", "x0", "s1", "s2", "s3", "x1", "w00", "w10", "x2", "w20", "w30", "x3", "w01"):
-            load(what)
+        ident = keep.tile([P, P], F32, name="ident")
+        make_identity(nc, ident[:])
 
-        cf_b = keep.tile([P, CELLS], BF16, name="cf_b")
-        lb_b = keep.tile([P, H], BF16, name="lb_b")
+        xs_t = keep.tile([P, PASSES, 4], F32, name="xs_t")
+        cf_c = keep.tile([P, TILES], BF16, name="cf_c")
+        lb_c = keep.tile([P, 4], BF16, name="lb_c")
         pb_t = keep.tile([P, GROUPS, 4], BF16, name="pb_t")
         ag_t = keep.tile([P, GROUPS, 4], BF16, name="ag_t")
         lg_t = keep.tile([P, GROUPS, 4], BF16, name="lg_t")
         lg_f = keep.tile([P, GROUPS, 4], F32, name="lg_f")
-        noise_t = keep.tile([P, CELLS // P, LATENT], BF16, name="noise_t")
-        nc.gpsimd.dma_start(out=pb_t[:], in_=pathway_bias.rearrange("(g p t) -> p g t", p=P, t=4))
-        nc.gpsimd.dma_start(out=ag_t[:], in_=activity_gain.rearrange("(g p t) -> p g t", p=P, t=4))
-        nc.gpsimd.dma_start(out=lg_t[:], in_=loading_gain.rearrange("(g p t) -> p g t", p=P, t=4))
+        cf_b = keep.tile([P, CELLS], F32, name="cf_b")
+        lb_b = keep.tile([P, H], F32, name="lb_b")
+        noise_t = keep.tile([P, TILES, LATENT], BF16, name="noise_t")
+        nc.scalar.dma_start(out=xs_t[:], in_=x_scale.rearrange("o (g p t) -> p (o g) t", p=P, t=4))
+        nc.scalar.dma_start(out=cf_c[:], in_=cell_factor.rearrange("(p i) -> p i", i=TILES))
+        nc.scalar.dma_start(out=lb_c[:], in_=latent_bias.rearrange("(n c) -> n c", c=4))
+        nc.scalar.dma_start(out=pb_t[:], in_=pathway_bias.rearrange("(g p t) -> p g t", p=P, t=4))
+        nc.scalar.dma_start(out=ag_t[:], in_=activity_gain.rearrange("(g p t) -> p g t", p=P, t=4))
+        nc.scalar.dma_start(out=lg_t[:], in_=loading_gain.rearrange("(g p t) -> p g t", p=P, t=4))
+        nc.scalar.activation(out=warm[:], in_=warm[:], func=ACT.Silu)
+        for what in FIRST_LOADS:
+            load(what)
         nc.gpsimd.tensor_copy(out=lg_f[:], in_=lg_t[:])
 
-        LATER = {0: ("x4", "w11"), 1: ("x5", "w21"), 2: ("x6", "w31"), 3: ("x7", "e0", "e1", "e2", "e3", "cf", "lb", "noise")}
-
-        xc = [keep.tile([P, PASSES, 512], U32, name=f"xc{h}", align_bytes=64) for h in range(HALVES)]
-        xs = [keep.tile([P, PASSES, 512], U8, name=f"xs{h}", align_bytes=64) for h in range(HALVES)]
+        xc = [keep.tile([P, PASSES, 256], U32, name=f"xc{pr}", align_bytes=64) for pr in range(4)]
+        xs = [keep.tile([P, PASSES, 256], U8, name=f"xs{pr}", align_bytes=64) for pr in range(4)]
         wc = {}
         ws = {}
         for g in range(PASSES):
@@ -340,94 +294,93 @@ def tile_pathway_latent_encoder_f5_kernel(
                 T[key] = pool.tile(shape, dt, name=tag, **kw)
             return T[key]
 
-        def P_(i, c):
-            n = {0: 4, 1: 2}.get(i, 1)
-            xw = get(work, "xw", ("xw", i), [P, GENES], BF16, align_bytes=64)
-            s = slice(c * GENES // n, (c + 1) * GENES // n)
-            nc.vector.tensor_tensor(out=xw[:, s], in0=x_raw[i][:, s].bitcast(F8), in1=scale_b[:, s], op=ALU.mult)
-            if c == n - 1 and i in LATER:
-                for what in LATER[i]:
-                    if what == "cf":
-                        nc.sync.dma_start(out=cf_b[:], in_=cell_factor.partition_broadcast(P))
-                    elif what == "lb":
-                        nc.sync.dma_start(out=lb_b[:], in_=latent_bias.partition_broadcast(P))
-                    elif what == "noise":
-                        nc.sync.dma_start(out=noise_t[:], in_=noise.rearrange("(t p) l -> p t l", p=P))
-                    else:
-                        load(what)
-
-        def Tp(i, gp):
-            bank = get(ps_tr, "tr", ("tr", i, gp), [P, 2, 2, P], F32)
-            words = T["xw", i][:].bitcast(F32)
-            for gi in range(2):
-                g = 2 * gp + gi
-                for u in range(2):
-                    nc.tensor.transpose(bank[:, gi, u, :], words[:, 256 * g + u : 256 * (g + 1) : 2], ident[:])
-
-        def Ts(i, gp):
-            h, mt = divmod(i, 4)
-            xg = get(xgp, "xg", ("xg", h, gp), [P, 2, 512, 4], BF16, align_bytes=64)
-            dst = xg[:].rearrange("p g m t -> p (g m t)").bitcast(F32).rearrange("p (g m u) -> p g m u", g=2, u=2)
-            nc.scalar.copy(out=dst[:, :, mt * P : (mt + 1) * P, :], in_=T["tr", i, gp][:].rearrange("p g u m -> p g m u"))
-
-        def XQ(h, g):
-            src = T["xg", h, g // 2][:, g % 2, :, :].rearrange("p m t -> p (m t)")
-            nc.vector.quantize_mx(out=xc[h][:, g, :].bitcast(FP8X4), scales=xs[h][:, g, :], in_=src)
-
-        def raw(u):
-            if u[0] == "w":
-                return w_raw[u[1], u[2]][:].rearrange("p j (m t) -> p j t m", t=4)
-            return e_raw[u[1]][:].rearrange("p j (t m) -> p j t m", t=4)
-
-        def Ip(k, g, jg, b):
-            u = (k, g, jg)
-            bank = get(ps_id, "idb", ("id", u, b), [P, 1024], BF16)
-            for i in range(2):
+        def CF(_):
+            for h in range(HALVES):
+                bank = get(ps_tr, "tr", ("cf", h), [P, 512], F32)
+                for i in range(4):
+                    nc.tensor.matmul(
+                        bank[:, i * P : (i + 1) * P],
+                        lhsT=cf_c[:, 4 * h + i : 4 * h + i + 1].to_broadcast([P, P]),
+                        rhs=ident_bf[:],
+                        start=True,
+                        stop=True,
+                    )
+                nc.scalar.copy(out=cf_b[:, h * 512 : (h + 1) * 512], in_=bank[:])
+            bank = get(ps_tr, "tr", ("lb",), [P, 512], F32)
+            for c in range(4):
                 nc.tensor.matmul(
-                    bank[:, i * 512 : (i + 1) * 512],
-                    lhsT=ident_bf[:],
-                    rhs=raw(u)[:, :, 2 * b + i, :].rearrange("p j m -> p m j"),
-                    start=True,
-                    stop=True,
+                    bank[:, c * P : (c + 1) * P], lhsT=lb_c[:, c : c + 1].to_broadcast([P, P]), rhs=ident_bf[:], start=True, stop=True
                 )
+            nc.scalar.copy(out=lb_b[:].rearrange("p (n c) -> p n c", c=4), in_=bank[:].rearrange("p (c n) -> p n c", c=4))
 
-        def Is(k, g, jg, b):
-            u = (k, g, jg)
-            dst = get(grp, "gr", ("gr", u), [P, 2048], BF16, align_bytes=64)
-            nc.scalar.copy(out=dst[:, b * 1024 : (b + 1) * 1024], in_=T["id", u, b][:])
+        def K(i):
+            pr, i2 = divmod(i, 2)
+            xw = get(xwp, "xw", ("xw", pr), [P, 2, GENES], BF16)
+            nc.scalar.copy(out=xw[:, i2, :], in_=x_raw[pr][:, i2, :].bitcast(F8))
+            for what in LOADS_AFTER.get(i, ()):
+                load(what)
+
+        def Tp(pr, g):
+            bank = get(ps_tr, "tr", ("x", pr, g), [P, 512], F32)
+            for i2 in range(2):
+                words = T["xw", pr][:, i2, :].bitcast(F32)
+                for u in range(2):
+                    nc.tensor.transpose(
+                        bank[:, u * 256 + i2 * P : u * 256 + (i2 + 1) * P], words[:, 256 * g + u : 256 * (g + 1) : 2], ident[:]
+                    )
+
+        def PP(pr, g):
+            xg = get(xgp, "xg", ("xg", pr), [P, PASSES, 1024], BF16, align_bytes=64)
+            nc.vector.tensor_tensor(
+                out=xg[:, g, :].rearrange("p (m u e) -> p m u e", u=2, e=2),
+                in0=T["x", pr, g][:].bitcast(BF16).rearrange("p (u m e) -> p m u e", u=2, e=2),
+                in1=xs_t[:, g, :].rearrange("p (u e) -> p u e", e=2).unsqueeze(1).to_broadcast([P, 256, 2, 2]),
+                op=ALU.mult,
+            )
+
+        def XQ(pr, k):
+            nc.vector.quantize_mx(
+                out=xc[pr][:, 2 * k : 2 * k + 2, :].rearrange("p g m -> p (g m)").bitcast(FP8X4),
+                scales=xs[pr][:, 2 * k : 2 * k + 2, :].rearrange("p g m -> p (g m)"),
+                in_=T["xg", pr][:, 2 * k : 2 * k + 2, :].rearrange("p g c -> p (g c)"),
+            )
 
         def D(k, g, jg):
-            dst = get(grp, "gr", ("gr", (k, g, jg)), [P, 2048], BF16, align_bytes=64)
+            u = (k, g, jg)
+            dst = get(grp, "gr", ("gr", u), [P, 2048], BF16, align_bytes=64)
             if k == "w":
-                nc.scalar.copy(out=dst[:].rearrange("p (t m j) -> p t m j", t=4, j=4), in_=raw((k, g, jg)).rearrange("p j t m -> p t m j"))
+                o = dst[:].rearrange("p (t m j) -> p m t j", t=4, j=4)
+                i = raws[u][:].rearrange("p j (m t) -> p m t j", t=4)
             else:
-                nc.scalar.copy(
-                    out=dst[:].rearrange("p (c i j) -> p c j i", i=4, j=4), in_=e_raw[g][:].rearrange("p j (c i) -> p c j i", i=4)
-                )
+                o = dst[:].rearrange("p (c i j) -> p c j i", i=4, j=4)
+                i = raws[u][:].rearrange("p j (c i) -> p c j i", i=4)
+            if u in ON_VECTOR:
+                nc.vector.tensor_copy(out=o, in_=i)
+            else:
+                nc.scalar.copy(out=o, in_=i)
 
         def WQ(k, g, jg):
             u = (k, g, jg)
             nc.vector.quantize_mx(out=wc[u][:].bitcast(FP8X4), scales=ws[u][:], in_=T["gr", u][:])
 
-        def mx(bank, t, jg, rhs, rhs_s):
+        def U(jg, hh, t):
+            h = hh[1]
             col = slice(t * P, (t + 1) * P)
-            for g in range(PASSES):
-                nc.tensor.matmul_mx(
-                    out=bank[:],
-                    lhsT=wc["w", g, jg][:, col].bitcast(FP8X4),
-                    lhsT_scale=ws["w", g, jg][:, col],
-                    rhs=rhs(g).bitcast(FP8X4),
-                    rhs_scale=rhs_s(g),
-                    start=(g == 0),
-                    stop=(g == PASSES - 1),
-                )
-
-        def U(jg, h, t):
             bank = get(ps_mx, "mx", ("u", jg, h, t), [P, 512], F32)
-            mx(bank, t, jg, lambda g: xc[h][:, g, :], lambda g: xs[h][:, g, :])
+            for k in range(2):
+                for g in range(PASSES):
+                    nc.tensor.matmul_mx(
+                        out=bank[:, k * 256 : (k + 1) * 256],
+                        lhsT=wc["w", g, jg][:, col].bitcast(FP8X4),
+                        lhsT_scale=ws["w", g, jg][:, col],
+                        rhs=xc[2 * h + k][:, g, :].bitcast(FP8X4),
+                        rhs_scale=xs[2 * h + k][:, g, :],
+                        start=(g == 0),
+                        stop=(g == PASSES - 1),
+                    )
 
         def C(jg, h, t):
-            y = get(work, "y", ("y", jg, h), [P, 4, 512], F32)
+            y = get(yp, "y", ("y", jg, h), [P, 4, 512], F32)
             nc.vector.tensor_tensor(out=y[:, t, :], in0=T["u", jg, h, t][:], in1=cf_b[:, h * 512 : (h + 1) * 512], op=ALU.mult)
 
         def SI(jg, h, t):
@@ -437,9 +390,9 @@ def tile_pathway_latent_encoder_f5_kernel(
         def G(jg, h):
             dst = get(grp, "gr", ("gr", ("a", jg, h)), [P, 2048], BF16, align_bytes=64)
             nc.vector.tensor_tensor(
-                out=dst[:].rearrange("p (m t) -> p m t", t=4),
-                in0=T["y", jg, h][:].rearrange("p t m -> p m t"),
-                in1=ag_t[:, jg, :].unsqueeze(1).to_broadcast([P, 512, 4]),
+                out=dst[:].rearrange("p (c i t) -> p c t i", i=4, t=4),
+                in0=T["y", jg, h][:].rearrange("p t (c i) -> p c t i", i=4),
+                in1=ag_t[:, jg, :].unsqueeze(1).unsqueeze(3).to_broadcast([P, P, 4, 4]),
                 op=ALU.mult,
             )
 
@@ -447,51 +400,69 @@ def tile_pathway_latent_encoder_f5_kernel(
             nc.vector.quantize_mx(out=ac[jg][h][:].bitcast(FP8X4), scales=asc[jg][h][:], in_=T["gr", ("a", jg, h)][:])
 
         def VM(jg, t):
+            col = slice(t * P, (t + 1) * P)
             bank = get(ps_mx, "mx", ("v", jg, t), [P, 512], F32)
-            mx(bank, t, jg, lambda g: wc["e", g, 0][:], lambda g: ws["e", g, 0][:])
+            for g in range(PASSES):
+                nc.tensor.matmul_mx(
+                    out=bank[:],
+                    lhsT=wc["w", g, jg][:, col].bitcast(FP8X4),
+                    lhsT_scale=ws["w", g, jg][:, col],
+                    rhs=wc["e", g, 0][:].bitcast(FP8X4),
+                    rhs_scale=ws["e", g, 0][:],
+                    start=(g == 0),
+                    stop=(g == PASSES - 1),
+                )
 
         def VS(jg, t):
             nc.scalar.activation(out=vl[jg][:, t, :], in_=T["v", jg, t][:], func=ACT.Copy, scale=lg_f[:, jg, t : t + 1])
 
         def VI(jg):
             dst = get(grp, "gr", ("gr", ("v", jg)), [P, 2048], BF16, align_bytes=64)
-            nc.scalar.copy(out=dst[:].rearrange("p (c i t) -> p c t i", i=4, t=4), in_=vl[jg][:].rearrange("p t (c i) -> p c t i", i=4))
+            nc.vector.tensor_copy(out=dst[:].rearrange("p (c i t) -> p c t i", i=4, t=4), in_=vl[jg][:].rearrange("p t (c i) -> p c t i", i=4))
 
         def VQ(jg):
             nc.vector.quantize_mx(out=vc[jg][:].bitcast(FP8X4), scales=vsc[jg][:], in_=T["gr", ("v", jg)][:])
 
-        def Q(mt, jg):
-            h, m = divmod(mt, 4)
-            rows = slice(m * P, (m + 1) * P)
-            bank = get(ps_mx, "mx", ("q", mt), [P, 512], F32)
-            nc.tensor.matmul_mx(
-                out=bank[:],
-                lhsT=ac[jg][h][:, rows].bitcast(FP8X4),
-                lhsT_scale=asc[jg][h][:, rows],
-                rhs=vc[jg][:].bitcast(FP8X4),
-                rhs_scale=vsc[jg][:],
-                start=(jg == 0),
-                stop=(jg == 1),
-            )
+        def Q(i):
+            h, k = divmod(i, 4)
+            cells = slice(k * P, (k + 1) * P)
+            bank = get(ps_mx, "mx", ("q", i), [P, 512], F32)
+            for jg in range(GROUPS):
+                nc.tensor.matmul_mx(
+                    out=bank[:],
+                    lhsT=ac[jg][h][:, cells].bitcast(FP8X4),
+                    lhsT_scale=asc[jg][h][:, cells],
+                    rhs=vc[jg][:].bitcast(FP8X4),
+                    rhs_scale=vsc[jg][:],
+                    start=(jg == 0),
+                    stop=(jg == GROUPS - 1),
+                )
 
-        def QB(mt):
-            qb = get(qbp, "qb", ("qb", mt), [P, H], F32)
-            nc.vector.tensor_tensor(out=qb[:], in0=T["q", mt][:], in1=lb_b[:], op=ALU.add)
-            nc.sync.dma_start(out=mu_out[mt * P : (mt + 1) * P, :], in_=qb[:, 0:LATENT])
+        mu_rows = mu_out.rearrange("(p i) l -> p i l", i=TILES)
+        sd_rows = sd_out.rearrange("(p i) l -> p i l", i=TILES)
+        z_rows = z_out.rearrange("(p i) l -> p i l", i=TILES)
 
-        def TH(mt):
-            qb = T["qb", mt]
-            sd = get(outs, "sd", ("sd", mt), [P, LATENT], F32)
-            nc.scalar.activation(out=sd[:], in_=qb[:, LATENT:H], func=ACT.Tanh)
+        def QB(i):
+            pr, i2 = divmod(i, 2)
+            qb = get(qbp, "qb", ("qb", pr), [P, 2, H], F32)
+            nc.vector.tensor_tensor(out=qb[:, i2, :], in0=T["q", i][:], in1=lb_b[:], op=ALU.add)
+
+        def TH(pr):
+            qb = T["qb", pr]
+            rows = slice(2 * pr, 2 * pr + 2)
+            nc.sync.dma_start(out=mu_rows[:, rows, :], in_=qb[:, :, 0:LATENT])
+            sd = get(outs, "sd", ("sd", pr), [P, 2, LATENT], F32)
+            nc.scalar.activation(out=sd[:], in_=qb[:, :, LATENT:H], func=ACT.Tanh)
             nc.scalar.activation(out=sd[:], in_=sd[:], func=ACT.Exp, scale=0.5)
-            nc.sync.dma_start(out=sd_out[mt * P : (mt + 1) * P, :], in_=sd[:])
+            nc.sync.dma_start(out=sd_rows[:, rows, :], in_=sd[:])
 
-        def Z(mt):
-            z = get(outs, "z", ("z", mt), [P, LATENT], F32)
-            nc.vector.tensor_tensor(out=z[:], in0=T["sd", mt][:], in1=noise_t[:, mt, :], op=ALU.mult)
-            nc.vector.tensor_tensor(out=z[:], in0=z[:], in1=T["qb", mt][:, 0:LATENT], op=ALU.add)
-            nc.sync.dma_start(out=z_out[mt * P : (mt + 1) * P, :], in_=z[:])
+        def Z(pr):
+            rows = slice(2 * pr, 2 * pr + 2)
+            z = get(outs, "z", ("z", pr), [P, 2, LATENT], F32)
+            nc.vector.tensor_tensor(out=z[:], in0=T["sd", pr][:], in1=noise_t[:, rows, :], op=ALU.mult)
+            nc.vector.tensor_tensor(out=z[:], in0=z[:], in1=T["qb", pr][:, :, 0:LATENT], op=ALU.add)
+            nc.sync.dma_start(out=z_rows[:, rows, :], in_=z[:])
 
-        steps = dict(P=P_, Tp=Tp, Ts=Ts, XQ=XQ, Ip=Ip, Is=Is, D=D, WQ=WQ, U=U, C=C, SI=SI, G=G, AQ=AQ, VM=VM, VS=VS, VI=VI, VQ=VQ, Q=Q, QB=QB, TH=TH, Z=Z)
+        steps = dict(CF=CF, K=K, Tp=Tp, PP=PP, XQ=XQ, D=D, WQ=WQ, U=U, C=C, SI=SI, G=G, AQ=AQ, VM=VM, VS=VS, VI=VI, VQ=VQ, Q=Q, QB=QB, TH=TH, Z=Z)
         for step in ORDER:
             steps[step[0]](*step[1:])

@@ -19,186 +19,264 @@ PASSES = GENES // 512
 GROUPS = PATHWAYS // 512
 HALVES = CELLS // 512
 TILES = CELLS // P
-TR = 2
-ON_VECTOR = {("w", 0, 0)}
-FIRST_LOADS = ("x0", "w00", "w10", "x1", "w20", "w30", "x2",)
-LOADS_AFTER = {1: ("w01", "w11", "x3", "w21", "w31",), 5: ("e0", "e1", "e2", "e3", "noise",)}
+TR = 4
+Z_ON_GPSIMD = (0, 1,)
+D_ENGINE = {("w", 0, 0): "V", ("w", 1, 0): "V", ("w", 2, 0): "S", ("w", 3, 0): "G", ("w", 0, 1): "S", ("w", 1, 1): "G", ("w", 2, 1): "V", ("w", 3, 1): "S", ("e", 0, 0): "G", ("e", 1, 0): "G", ("e", 2, 0): "G", ("e", 3, 0): "S"}
+FIRST_LOADS = ("w00", "x0", "w10", "w20", "w30", "x1", "e0", "x2", "e2", "e3", "e1",)
+LOADS_AFTER = {1: ("x3", "w01", "w11", "w21", "w31", "noise",)}
 FLOPS = 2 * CELLS * GENES * PATHWAYS + 2 * GENES * PATHWAYS * H + 2 * CELLS * PATHWAYS * H
 
 ORDER = [
-    ("K", 0),
-    ("K", 1),
     ("D", "w", 0, 0),
-    ("CF", 0),
-    ("Tp", 0, 0),
+    ("K", 0),
     ("WQ", "w", 0, 0),
-    ("Tp", 0, 1),
-    ("PP", 0, 0),
-    ("K", 2),
-    ("PP", 0, 1),
-    ("Tp", 0, 2),
-    ("K", 3),
-    ("PP", 0, 2),
-    ("Tp", 0, 3),
     ("D", "w", 1, 0),
-    ("XQ", 0, 0),
-    ("Tp", 1, 0),
-    ("PP", 0, 3),
-    ("PP", 1, 0),
-    ("Tp", 1, 3),
-    ("K", 4),
-    ("XQ", 0, 1),
-    ("Tp", 1, 2),
-    ("K", 5),
-    ("WQ", "w", 1, 0),
-    ("PP", 1, 3),
+    ("K", 1),
     ("D", "w", 2, 0),
+    ("WQ", "w", 1, 0),
+    ("Tp", 0, 0),
+    ("Tp", 0, 2),
+    ("Dg", "w", 3, 0, 3),
+    ("PP", 0, 0),
+    ("Tp", 0, 1),
+    ("Dg", "w", 3, 0, 2),
+    ("Tp", 0, 3),
+    ("PP", 0, 1),
+    ("Dg", "w", 3, 0, 1),
+    ("K", 3),
+    ("PP", 0, 3),
+    ("Dg", "e", 0, 0, 0),
+    ("Dg", "e", 0, 0, 3),
+    ("K", 2),
+    ("PP", 0, 2),
+    ("Dg", "e", 0, 0, 1),
+    ("XQ", 0, 0),
+    ("K", 5),
+    ("Tp", 1, 3),
+    ("XQ", 0, 1),
+    ("U", 0, 0, 0, 0),
+    ("U", 0, 0, 0, 1),
+    ("PP", 1, 3),
+    ("Dg", "e", 2, 0, 1),
+    ("U", 0, 0, 1, 0),
+    ("D", "e", 3, 0),
+    ("U", 0, 0, 1, 1),
+    ("Tp", 1, 2),
+    ("Dg", "e", 2, 0, 0),
+    ("Tp", 1, 0),
     ("PP", 1, 2),
-    ("Tp", 2, 0),
-    ("PP", 2, 0),
-    ("Tp", 2, 2),
-    ("D", "w", 3, 0),
+    ("Dg", "e", 2, 0, 3),
+    ("Tp", 1, 1),
+    ("Dg", "e", 2, 0, 2),
+    ("PP", 1, 1),
+    ("K", 7),
+    ("Dg", "e", 0, 0, 2),
+    ("PP", 1, 0),
+    ("Dg", "w", 3, 0, 0),
+    ("K", 4),
     ("XQ", 1, 1),
+    ("WQ", "w", 3, 0),
+    ("K", 6),
+    ("Tp", 2, 1),
+    ("XQ", 1, 0),
     ("Tp", 2, 3),
     ("WQ", "w", 2, 0),
-    ("PP", 2, 2),
+    ("Tp", 2, 0),
     ("D", "w", 0, 1),
-    ("PP", 2, 3),
-    ("Tp", 1, 1),
-    ("WQ", "w", 3, 0),
-    ("Tp", 2, 1),
-    ("PP", 1, 1),
-    ("K", 6),
-    ("WQ", "w", 0, 1),
-    ("XQ", 1, 0),
-    ("K", 7),
-    ("XQ", 2, 1),
-    ("U", 0, ("h", 0), 0),
-    ("PP", 2, 1),
-    ("D", "w", 1, 1),
-    ("Tp", 3, 2),
-    ("C", 0, 0, 0),
-    ("Tp", 3, 0),
-    ("XQ", 2, 0),
-    ("U", 0, ("h", 0), 1),
-    ("PP", 3, 2),
-    ("SI", 0, 0, 0),
-    ("U", 0, ("h", 0), 2),
-    ("D", "w", 2, 1),
-    ("WQ", "w", 1, 1),
-    ("PP", 3, 0),
-    ("Tp", 3, 1),
-    ("U", 0, ("h", 0), 3),
-    ("PP", 3, 1),
-    ("D", "w", 3, 1),
     ("Tp", 3, 3),
-    ("WQ", "w", 2, 1),
-    ("XQ", 3, 0),
+    ("PP", 2, 3),
+    ("Dg", "w", 1, 1, 0),
+    ("U", 0, 0, 0, 2),
+    ("Dg", "w", 1, 1, 2),
+    ("U", 0, 0, 0, 3),
+    ("U", 0, 0, 3, 0),
+    ("PP", 2, 0),
+    ("U", 0, 0, 3, 1),
+    ("Dg", "w", 1, 1, 1),
+    ("Tp", 3, 0),
+    ("U", 0, 0, 1, 2),
     ("PP", 3, 3),
-    ("D", "e", 0, 0),
-    ("C", 0, 0, 1),
-    ("WQ", "w", 3, 1),
-    ("XQ", 3, 1),
-    ("U", 1, ("h", 0), 0),
-    ("C", 0, 0, 2),
-    ("C", 0, 0, 3),
+    ("Dg", "w", 1, 1, 3),
+    ("CS", 0, 0, 0),
+    ("U", 0, 0, 1, 3),
+    ("U", 0, 0, 3, 2),
+    ("CS", 0, 0, 1),
+    ("U", 0, 0, 2, 0),
+    ("WQ", "w", 0, 1),
+    ("U", 0, 0, 2, 1),
+    ("CF", 0),
+    ("U", 0, 0, 2, 2),
+    ("U", 0, 0, 2, 3),
+    ("D", "w", 2, 1),
+    ("U", 1, 0, 1, 0),
+    ("CS", 0, 0, 2),
+    ("U", 1, 0, 3, 0),
+    ("U", 0, 0, 3, 3),
+    ("U", 1, 0, 2, 0),
+    ("CS", 0, 0, 3),
+    ("Tp", 2, 2),
+    ("WQ", "w", 1, 1),
+    ("UT", 0, 0, 0),
+    ("WQ", "w", 2, 1),
+    ("D", "w", 3, 1),
+    ("U", 1, 0, 1, 1),
+    ("PP", 2, 2),
+    ("Dg", "e", 1, 0, 3),
+    ("U", 1, 0, 2, 1),
+    ("U", 1, 0, 0, 0),
+    ("U", 1, 0, 0, 1),
+    ("Dg", "e", 1, 0, 1),
+    ("U", 1, 0, 0, 2),
+    ("U", 1, 0, 2, 2),
+    ("PP", 3, 0),
+    ("UT", 0, 0, 1),
+    ("Dg", "e", 1, 0, 2),
+    ("U", 1, 0, 3, 1),
+    ("U", 1, 0, 3, 2),
     ("SI", 0, 0, 1),
-    ("U", 1, ("h", 0), 1),
-    ("WQ", "e", 0, 0),
+    ("PP", 2, 1),
+    ("Dg", "e", 1, 0, 0),
+    ("UT", 0, 0, 2),
+    ("SI", 0, 0, 0),
+    ("Tp", 3, 2),
+    ("WQ", "w", 3, 1),
+    ("UT", 0, 0, 3),
     ("SI", 0, 0, 2),
-    ("C", 1, 0, 0),
-    ("U", 1, ("h", 0), 2),
+    ("Tp", 3, 1),
     ("SI", 0, 0, 3),
-    ("C", 1, 0, 1),
+    ("XQ", 2, 0),
+    ("U", 1, 0, 0, 3),
+    ("U", 1, 0, 3, 3),
+    ("PP", 3, 1),
+    ("CS", 1, 0, 0),
+    ("U", 1, 0, 2, 3),
+    ("U", 1, 0, 1, 2),
+    ("CS", 1, 0, 2),
+    ("U", 1, 1, 0, 0),
+    ("U", 1, 1, 0, 1),
+    ("PP", 3, 2),
+    ("U", 1, 0, 1, 3),
+    ("CS", 1, 0, 3),
+    ("U", 0, 1, 0, 0),
+    ("U", 0, 1, 0, 1),
+    ("CS", 1, 0, 1),
+    ("U", 0, 1, 1, 0),
+    ("XQ", 3, 0),
+    ("U", 0, 1, 1, 1),
+    ("U", 1, 1, 1, 0),
+    ("UT", 1, 0, 0),
+    ("XQ", 2, 1),
+    ("UT", 1, 0, 2),
     ("SI", 1, 0, 0),
-    ("G", 0, 0),
-    ("U", 1, ("h", 0), 3),
-    ("SI", 1, 0, 1),
-    ("D", "e", 1, 0),
-    ("U", 0, ("h", 1), 0),
-    ("C", 1, 0, 2),
-    ("U", 0, ("h", 1), 1),
-    ("C", 1, 0, 3),
-    ("SI", 1, 0, 2),
-    ("C", 0, 1, 0),
-    ("U", 0, ("h", 1), 2),
-    ("WQ", "e", 1, 0),
-    ("SI", 1, 0, 3),
-    ("U", 0, ("h", 1), 3),
-    ("AQ", 0, 0),
-    ("SI", 0, 1, 0),
-    ("D", "e", 2, 0),
-    ("G", 1, 0),
-    ("U", 1, ("h", 1), 0),
-    ("U", 1, ("h", 1), 1),
-    ("C", 0, 1, 2),
-    ("D", "e", 3, 0),
-    ("U", 1, ("h", 1), 2),
-    ("WQ", "e", 2, 0),
-    ("C", 0, 1, 3),
-    ("U", 1, ("h", 1), 3),
-    ("C", 1, 1, 0),
-    ("C", 1, 1, 1),
-    ("C", 1, 1, 2),
-    ("SI", 0, 1, 3),
     ("WQ", "e", 3, 0),
-    ("SI", 1, 1, 0),
-    ("C", 1, 1, 3),
-    ("SI", 1, 1, 1),
+    ("UT", 1, 0, 3),
+    ("UT", 1, 0, 1),
+    ("SI", 1, 0, 2),
+    ("XQ", 3, 1),
+    ("U", 0, 1, 0, 2),
+    ("SI", 1, 0, 1),
+    ("U", 0, 1, 0, 3),
+    ("WQ", "e", 0, 0),
+    ("U", 1, 1, 1, 1),
+    ("U", 1, 1, 0, 2),
+    ("CS", 0, 1, 0),
+    ("WQ", "e", 1, 0),
+    ("U", 1, 1, 0, 3),
+    ("U", 0, 1, 1, 2),
+    ("CS", 1, 1, 0),
+    ("U", 0, 1, 2, 0),
+    ("WQ", "e", 2, 0),
+    ("U", 0, 1, 2, 1),
+    ("SI", 1, 0, 3),
+    ("U", 0, 1, 3, 0),
+    ("G", 0, 0),
+    ("U", 0, 1, 1, 3),
+    ("U", 0, 1, 3, 1),
+    ("CS", 0, 1, 1),
+    ("U", 0, 1, 3, 2),
+    ("U", 0, 1, 2, 2),
     ("VM", 0, 3),
-    ("AQ", 1, 0),
-    ("SI", 1, 1, 2),
-    ("C", 0, 1, 1),
-    ("VM", 0, 0),
-    ("SI", 1, 1, 3),
-    ("VS", 0, 3),
-    ("G", 1, 1),
-    ("VM", 0, 1),
-    ("SI", 0, 1, 1),
-    ("SI", 0, 1, 2),
-    ("VM", 0, 2),
-    ("VS", 0, 1),
-    ("G", 0, 1),
-    ("VS", 0, 0),
-    ("VM", 1, 0),
-    ("VS", 0, 2),
+    ("G", 1, 0),
+    ("U", 0, 1, 2, 3),
+    ("U", 1, 1, 1, 2),
+    ("CS", 0, 1, 2),
+    ("U", 0, 1, 3, 3),
+    ("U", 1, 1, 1, 3),
+    ("CS", 0, 1, 3),
     ("VM", 1, 1),
-    ("VS", 1, 0),
-    ("VI", 0),
-    ("VM", 1, 2),
-    ("VS", 1, 1),
-    ("AQ", 1, 1),
+    ("CS", 1, 1, 1),
+    ("VX", 0, 3),
+    ("UT", 0, 1, 0),
+    ("AQ", 0, 0),
+    ("UT", 0, 1, 1),
+    ("SI", 0, 1, 0),
+    ("UT", 0, 1, 2),
+    ("AQ", 1, 0),
+    ("UT", 0, 1, 3),
+    ("SI", 0, 1, 1),
     ("VM", 1, 3),
-    ("VS", 1, 2),
-    ("VQ", 0),
+    ("VX", 1, 1),
+    ("SI", 0, 1, 2),
+    ("SI", 0, 1, 3),
+    ("U", 1, 1, 2, 0),
+    ("VX", 1, 3),
+    ("U", 1, 1, 2, 1),
+    ("U", 1, 1, 2, 2),
+    ("G", 0, 1),
+    ("U", 1, 1, 2, 3),
+    ("VM", 0, 0),
+    ("CS", 1, 1, 2),
+    ("VM", 1, 0),
+    ("VX", 0, 0),
+    ("VM", 1, 2),
     ("AQ", 0, 1),
-    ("VS", 1, 3),
-    ("VI", 1),
+    ("VX", 1, 0),
+    ("U", 1, 1, 3, 0),
+    ("VX", 1, 2),
+    ("U", 1, 1, 3, 1),
+    ("VM", 0, 1),
     ("VQ", 1),
-    ("Q", 0),
+    ("U", 1, 1, 3, 2),
+    ("VX", 0, 1),
+    ("U", 1, 1, 3, 3),
+    ("VM", 0, 2),
+    ("CS", 1, 1, 3),
+    ("UT", 1, 1, 3),
+    ("VX", 0, 2),
+    ("UT", 1, 1, 0),
+    ("SI", 1, 1, 3),
+    ("UT", 1, 1, 2),
+    ("VQ", 0),
+    ("UT", 1, 1, 1),
+    ("SI", 1, 1, 0),
     ("Q", 1),
-    ("QB", 0),
-    ("Q", 2),
+    ("SI", 1, 1, 1),
+    ("Q", 0),
+    ("SI", 1, 1, 2),
     ("QB", 1),
+    ("Q", 2),
+    ("QB", 0),
     ("Q", 3),
-    ("QB", 2),
+    ("G", 1, 1),
     ("TH", 0),
-    ("Q", 4),
     ("QB", 3),
-    ("Q", 5),
-    ("QB", 4),
-    ("Q", 6),
-    ("QB", 5),
-    ("Q", 7),
-    ("QB", 6),
-    ("QB", 7),
-    ("TH", 1),
+    ("AQ", 1, 1),
+    ("QB", 2),
     ("Z", 0),
+    ("Q", 6),
+    ("Q", 7),
+    ("TH", 1),
+    ("QB", 6),
+    ("Q", 5),
+    ("QB", 7),
+    ("Q", 4),
+    ("QB", 5),
     ("TH", 3),
     ("Z", 1),
+    ("QB", 4),
     ("TH", 2),
-    ("Z", 3),
     ("Z", 2),
+    ("Z", 3),
 ]
 
 
@@ -212,8 +290,9 @@ def tile_pathway_latent_encoder_f5_kernel(
         xwp = ctx.enter_context(tc.tile_pool(name="xwp", bufs=2))
         xgp = ctx.enter_context(tc.tile_pool(name="xgp", bufs=2))
         yp = ctx.enter_context(tc.tile_pool(name="yp", bufs=2))
+        uyp = ctx.enter_context(tc.tile_pool(name="uyp", bufs=2))
         grp = ctx.enter_context(tc.tile_pool(name="grp", bufs=5))
-        outs = ctx.enter_context(tc.tile_pool(name="outs", bufs=3))
+        outs = ctx.enter_context(tc.tile_pool(name="outs", bufs=2))
         qbp = ctx.enter_context(tc.tile_pool(name="qbp", bufs=4))
         rawp = ctx.enter_context(tc.tile_pool(name="rawp", bufs=10))
         ps_tr = ctx.enter_context(tc.psum_pool(name="ps_tr", bufs=TR))
@@ -256,8 +335,7 @@ def tile_pathway_latent_encoder_f5_kernel(
         pb_t = keep.tile([P, GROUPS, 4], BF16, name="pb_t")
         ag_t = keep.tile([P, GROUPS, 4], BF16, name="ag_t")
         lg_t = keep.tile([P, GROUPS, 4], BF16, name="lg_t")
-        lg_f = keep.tile([P, GROUPS, 4], F32, name="lg_f")
-        cf_b = keep.tile([P, CELLS], F32, name="cf_b")
+        cf_f = keep.tile([P, TILES], F32, name="cf_f")
         lb_b = keep.tile([P, H], F32, name="lb_b")
         noise_t = keep.tile([P, TILES, LATENT], BF16, name="noise_t")
         nc.scalar.dma_start(out=xs_t[:], in_=x_scale.rearrange("o (g p t) -> p (o g) t", p=P, t=4))
@@ -269,7 +347,7 @@ def tile_pathway_latent_encoder_f5_kernel(
         nc.scalar.activation(out=warm[:], in_=warm[:], func=ACT.Silu)
         for what in FIRST_LOADS:
             load(what)
-        nc.gpsimd.tensor_copy(out=lg_f[:], in_=lg_t[:])
+        nc.gpsimd.tensor_copy(out=cf_f[:], in_=cf_c[:])
 
         xc = [keep.tile([P, PASSES, 256], U32, name=f"xc{pr}", align_bytes=64) for pr in range(4)]
         xs = [keep.tile([P, PASSES, 256], U8, name=f"xs{pr}", align_bytes=64) for pr in range(4)]
@@ -285,7 +363,6 @@ def tile_pathway_latent_encoder_f5_kernel(
         asc = [[keep.tile([P, 512], U8, name=f"asc{jg}{h}", align_bytes=64) for h in range(HALVES)] for jg in range(GROUPS)]
         vc = [keep.tile([P, H], U32, name=f"vc{jg}", align_bytes=64) for jg in range(GROUPS)]
         vsc = [keep.tile([P, H], U8, name=f"vsc{jg}", align_bytes=64) for jg in range(GROUPS)]
-        vl = [keep.tile([P, 4, 512], BF16, name=f"vl{jg}") for jg in range(GROUPS)]
 
         T = {}
 
@@ -295,17 +372,6 @@ def tile_pathway_latent_encoder_f5_kernel(
             return T[key]
 
         def CF(_):
-            for h in range(HALVES):
-                bank = get(ps_tr, "tr", ("cf", h), [P, 512], F32)
-                for i in range(4):
-                    nc.tensor.matmul(
-                        bank[:, i * P : (i + 1) * P],
-                        lhsT=cf_c[:, 4 * h + i : 4 * h + i + 1].to_broadcast([P, P]),
-                        rhs=ident_bf[:],
-                        start=True,
-                        stop=True,
-                    )
-                nc.scalar.copy(out=cf_b[:, h * 512 : (h + 1) * 512], in_=bank[:])
             bank = get(ps_tr, "tr", ("lb",), [P, 512], F32)
             for c in range(4):
                 nc.tensor.matmul(
@@ -349,43 +415,58 @@ def tile_pathway_latent_encoder_f5_kernel(
             u = (k, g, jg)
             dst = get(grp, "gr", ("gr", u), [P, 2048], BF16, align_bytes=64)
             if k == "w":
-                o = dst[:].rearrange("p (t m j) -> p m t j", t=4, j=4)
-                i = raws[u][:].rearrange("p j (m t) -> p m t j", t=4)
+                o = dst[:].rearrange("p (t m j) -> p m j t", t=4, j=4)
+                i = raws[u][:].rearrange("p j (m t) -> p m j t", t=4)
             else:
                 o = dst[:].rearrange("p (c i j) -> p c j i", i=4, j=4)
                 i = raws[u][:].rearrange("p j (c i) -> p c j i", i=4)
-            if u in ON_VECTOR:
+            if D_ENGINE[u] == "V":
                 nc.vector.tensor_copy(out=o, in_=i)
             else:
                 nc.scalar.copy(out=o, in_=i)
+
+        def Dg(k, g, jg, b):
+            u = (k, g, jg)
+            dst = get(grp, "gr", ("gr", u), [P, 2048], BF16, align_bytes=64)
+            if k == "w":
+                i = raws[u][:].rearrange("p j (m t) -> p t m j", t=4)[:, b, :, :]
+            else:
+                i = raws[u][:, :, b * P : (b + 1) * P].rearrange("p j c -> p c j")
+            nc.gpsimd.tensor_scalar(
+                out=dst[:, b * 512 : (b + 1) * 512].rearrange("p (m j) -> p m j", j=4), in0=i, scalar1=1.0, scalar2=0.0, op0=ALU.mult, op1=ALU.add
+            )
 
         def WQ(k, g, jg):
             u = (k, g, jg)
             nc.vector.quantize_mx(out=wc[u][:].bitcast(FP8X4), scales=ws[u][:], in_=T["gr", u][:])
 
-        def U(jg, hh, t):
-            h = hh[1]
-            col = slice(t * P, (t + 1) * P)
-            bank = get(ps_mx, "mx", ("u", jg, h, t), [P, 512], F32)
-            for k in range(2):
-                for g in range(PASSES):
-                    nc.tensor.matmul_mx(
-                        out=bank[:, k * 256 : (k + 1) * 256],
-                        lhsT=wc["w", g, jg][:, col].bitcast(FP8X4),
-                        lhsT_scale=ws["w", g, jg][:, col],
-                        rhs=xc[2 * h + k][:, g, :].bitcast(FP8X4),
-                        rhs_scale=xs[2 * h + k][:, g, :],
-                        start=(g == 0),
-                        stop=(g == PASSES - 1),
-                    )
+        def U(jg, h, k, g):
+            pr, i2 = divmod(4 * h + k, 2)
+            bank = get(ps_mx, "mx", ("u", jg, h, k), [P, 512], F32)
+            nc.tensor.matmul_mx(
+                out=bank[:],
+                lhsT=xc[pr][:, g, i2 * P : (i2 + 1) * P].bitcast(FP8X4),
+                lhsT_scale=xs[pr][:, g, i2 * P : (i2 + 1) * P],
+                rhs=wc["w", g, jg][:].bitcast(FP8X4),
+                rhs_scale=ws["w", g, jg][:],
+                start=(g == 0),
+                stop=(g == PASSES - 1),
+            )
 
-        def C(jg, h, t):
-            y = get(yp, "y", ("y", jg, h), [P, 4, 512], F32)
-            nc.vector.tensor_tensor(out=y[:, t, :], in0=T["u", jg, h, t][:], in1=cf_b[:, h * 512 : (h + 1) * 512], op=ALU.mult)
+        def CS(jg, h, k):
+            uy = get(uyp, "uy", ("uy", jg, h), [P, 4, 512], F32)
+            i = 4 * h + k
+            nc.scalar.activation(out=uy[:, k, :], in_=T["u", jg, h, k][:], func=ACT.Copy, scale=cf_f[:, i : i + 1])
+
+        def UT(jg, h, t):
+            bank = get(ps_tr, "tr", ("y", jg, h, t), [P, 512], F32)
+            for k in range(4):
+                nc.tensor.transpose(bank[:, k * P : (k + 1) * P], T["uy", jg, h][:, k, t * P : (t + 1) * P], ident[:])
+            T["ut", jg, h, t] = bank
 
         def SI(jg, h, t):
-            y = T["y", jg, h]
-            nc.scalar.activation(out=y[:, t, :], in_=y[:, t, :], func=ACT.Silu, bias=pb_t[:, jg, t : t + 1])
+            y = get(yp, "y", ("y", jg, h), [P, 4, 512], F32)
+            nc.scalar.activation(out=y[:, t, :], in_=T["ut", jg, h, t][:], func=ACT.Silu, bias=pb_t[:, jg, t : t + 1])
 
         def G(jg, h):
             dst = get(grp, "gr", ("gr", ("a", jg, h)), [P, 2048], BF16, align_bytes=64)
@@ -399,26 +480,30 @@ def tile_pathway_latent_encoder_f5_kernel(
         def AQ(jg, h):
             nc.vector.quantize_mx(out=ac[jg][h][:].bitcast(FP8X4), scales=asc[jg][h][:], in_=T["gr", ("a", jg, h)][:])
 
-        def VM(jg, t):
-            col = slice(t * P, (t + 1) * P)
-            bank = get(ps_mx, "mx", ("v", jg, t), [P, 512], F32)
-            for g in range(PASSES):
-                nc.tensor.matmul_mx(
-                    out=bank[:],
-                    lhsT=wc["w", g, jg][:, col].bitcast(FP8X4),
-                    lhsT_scale=ws["w", g, jg][:, col],
-                    rhs=wc["e", g, 0][:].bitcast(FP8X4),
-                    rhs_scale=ws["e", g, 0][:],
-                    start=(g == 0),
-                    stop=(g == PASSES - 1),
-                )
+        def VM(jg, c):
+            cols = slice(c * P, (c + 1) * P)
+            bank = get(ps_mx, "mx", ("v", jg, c), [P, 512], F32)
+            for t in range(4):
+                col = slice(t * P, (t + 1) * P)
+                for g in range(PASSES):
+                    nc.tensor.matmul_mx(
+                        out=bank[:, t * P : (t + 1) * P],
+                        lhsT=wc["w", g, jg][:, col].bitcast(FP8X4),
+                        lhsT_scale=ws["w", g, jg][:, col],
+                        rhs=wc["e", g, 0][:, cols].bitcast(FP8X4),
+                        rhs_scale=ws["e", g, 0][:, cols],
+                        start=(g == 0),
+                        stop=(g == PASSES - 1),
+                    )
 
-        def VS(jg, t):
-            nc.scalar.activation(out=vl[jg][:, t, :], in_=T["v", jg, t][:], func=ACT.Copy, scale=lg_f[:, jg, t : t + 1])
-
-        def VI(jg):
+        def VX(jg, c):
             dst = get(grp, "gr", ("gr", ("v", jg)), [P, 2048], BF16, align_bytes=64)
-            nc.vector.tensor_copy(out=dst[:].rearrange("p (c i t) -> p c t i", i=4, t=4), in_=vl[jg][:].rearrange("p t (c i) -> p c t i", i=4))
+            nc.vector.tensor_tensor(
+                out=dst[:, c * 512 : (c + 1) * 512].rearrange("p (n t) -> p n t", t=4),
+                in0=T["v", jg, c][:].rearrange("p (t n) -> p n t", t=4),
+                in1=lg_t[:, jg, :].unsqueeze(1).to_broadcast([P, P, 4]),
+                op=ALU.mult,
+            )
 
         def VQ(jg):
             nc.vector.quantize_mx(out=vc[jg][:].bitcast(FP8X4), scales=vsc[jg][:], in_=T["gr", ("v", jg)][:])
@@ -459,10 +544,11 @@ def tile_pathway_latent_encoder_f5_kernel(
         def Z(pr):
             rows = slice(2 * pr, 2 * pr + 2)
             z = get(outs, "z", ("z", pr), [P, 2, LATENT], F32)
-            nc.vector.tensor_tensor(out=z[:], in0=T["sd", pr][:], in1=noise_t[:, rows, :], op=ALU.mult)
-            nc.vector.tensor_tensor(out=z[:], in0=z[:], in1=T["qb", pr][:, :, 0:LATENT], op=ALU.add)
+            eng = nc.gpsimd if pr in Z_ON_GPSIMD else nc.vector
+            eng.tensor_tensor(out=z[:], in0=T["sd", pr][:], in1=noise_t[:, rows, :], op=ALU.mult)
+            eng.tensor_tensor(out=z[:], in0=z[:], in1=T["qb", pr][:, :, 0:LATENT], op=ALU.add)
             nc.sync.dma_start(out=z_rows[:, rows, :], in_=z[:])
 
-        steps = dict(CF=CF, K=K, Tp=Tp, PP=PP, XQ=XQ, D=D, WQ=WQ, U=U, C=C, SI=SI, G=G, AQ=AQ, VM=VM, VS=VS, VI=VI, VQ=VQ, Q=Q, QB=QB, TH=TH, Z=Z)
+        steps = dict(CF=CF, Dg=Dg, K=K, Tp=Tp, PP=PP, XQ=XQ, D=D, WQ=WQ, U=U, SI=SI, G=G, AQ=AQ, CS=CS, UT=UT, VM=VM, VX=VX, VQ=VQ, Q=Q, QB=QB, TH=TH, Z=Z)
         for step in ORDER:
             steps[step[0]](*step[1:])

@@ -20,261 +20,191 @@ GROUPS = PATHWAYS // 512
 HALVES = CELLS // 512
 TILES = CELLS // P
 TR = 4
+TURNED = {(0, 0), (0, 1)}
 Z_ON_GPSIMD = (0, 1,)
-D_ENGINE = {("w", 0, 0): "V", ("w", 1, 0): "V", ("w", 2, 0): "S", ("w", 3, 0): "G", ("w", 0, 1): "S", ("w", 1, 1): "G", ("w", 2, 1): "V", ("w", 3, 1): "S", ("e", 0, 0): "G", ("e", 1, 0): "G", ("e", 2, 0): "G", ("e", 3, 0): "S"}
-FIRST_LOADS = ("w00", "x0", "w10", "w20", "w30", "x1", "e0", "x2", "e2", "e3", "e1",)
-LOADS_AFTER = {1: ("x3", "w01", "w11", "w21", "w31", "noise",)}
+D_ENGINE = {("w", 0, 0): "V", ("w", 1, 0): "V", ("w", 2, 0): "V", ("w", 3, 0): "S", ("w", 0, 1): "S", ("w", 1, 1): "S", ("w", 2, 1): "S", ("w", 3, 1): "S", ("e", 0, 0): "S", ("e", 1, 0): "S", ("e", 2, 0): "S", ("e", 3, 0): "S"}
+FIRST_LOADS = ("x0", "w00", "w10", "x1", "w20", "w30", "w01", "x2", "w11", "w21",)
+LOADS_AFTER = {0: ("x3", "w31",), 3: ("e2", "e0",), 4: ("e3", "noise",), 5: ("e1",)}
 FLOPS = 2 * CELLS * GENES * PATHWAYS + 2 * GENES * PATHWAYS * H + 2 * CELLS * PATHWAYS * H
 
 ORDER = [
+    ("K", 1),
     ("D", "w", 0, 0),
     ("K", 0),
-    ("WQ", "w", 0, 0),
-    ("D", "w", 1, 0),
-    ("K", 1),
-    ("D", "w", 2, 0),
-    ("WQ", "w", 1, 0),
-    ("Tp", 0, 0),
-    ("Tp", 0, 2),
-    ("Dg", "w", 3, 0, 3),
-    ("PP", 0, 0),
+    ("CF", 0),
     ("Tp", 0, 1),
-    ("Dg", "w", 3, 0, 2),
+    ("D", "w", 1, 0),
+    ("Tp", 0, 0),
     ("Tp", 0, 3),
     ("PP", 0, 1),
-    ("Dg", "w", 3, 0, 1),
     ("K", 3),
-    ("PP", 0, 3),
-    ("Dg", "e", 0, 0, 0),
-    ("Dg", "e", 0, 0, 3),
+    ("Tp", 0, 2),
+    ("WQ", "w", 0, 0),
     ("K", 2),
-    ("PP", 0, 2),
-    ("Dg", "e", 0, 0, 1),
-    ("XQ", 0, 0),
-    ("K", 5),
-    ("Tp", 1, 3),
-    ("XQ", 0, 1),
-    ("U", 0, 0, 0, 0),
-    ("U", 0, 0, 0, 1),
-    ("PP", 1, 3),
-    ("Dg", "e", 2, 0, 1),
-    ("U", 0, 0, 1, 0),
-    ("D", "e", 3, 0),
-    ("U", 0, 0, 1, 1),
-    ("Tp", 1, 2),
-    ("Dg", "e", 2, 0, 0),
-    ("Tp", 1, 0),
-    ("PP", 1, 2),
-    ("Dg", "e", 2, 0, 3),
+    ("PP", 0, 0),
+    ("D", "w", 3, 0),
     ("Tp", 1, 1),
-    ("Dg", "e", 2, 0, 2),
-    ("PP", 1, 1),
-    ("K", 7),
-    ("Dg", "e", 0, 0, 2),
+    ("PP", 0, 3),
+    ("Tp", 1, 2),
+    ("PP", 1, 2),
+    ("Tp", 1, 0),
+    ("K", 5),
     ("PP", 1, 0),
-    ("Dg", "w", 3, 0, 0),
-    ("K", 4),
-    ("XQ", 1, 1),
-    ("WQ", "w", 3, 0),
-    ("K", 6),
-    ("Tp", 2, 1),
-    ("XQ", 1, 0),
-    ("Tp", 2, 3),
-    ("WQ", "w", 2, 0),
-    ("Tp", 2, 0),
+    ("Tp", 1, 3),
     ("D", "w", 0, 1),
-    ("Tp", 3, 3),
-    ("PP", 2, 3),
-    ("Dg", "w", 1, 1, 0),
-    ("U", 0, 0, 0, 2),
-    ("Dg", "w", 1, 1, 2),
-    ("U", 0, 0, 0, 3),
-    ("U", 0, 0, 3, 0),
-    ("PP", 2, 0),
-    ("U", 0, 0, 3, 1),
-    ("Dg", "w", 1, 1, 1),
-    ("Tp", 3, 0),
-    ("U", 0, 0, 1, 2),
-    ("PP", 3, 3),
-    ("Dg", "w", 1, 1, 3),
-    ("CS", 0, 0, 0),
-    ("U", 0, 0, 1, 3),
-    ("U", 0, 0, 3, 2),
-    ("CS", 0, 0, 1),
-    ("U", 0, 0, 2, 0),
-    ("WQ", "w", 0, 1),
-    ("U", 0, 0, 2, 1),
-    ("CF", 0),
-    ("U", 0, 0, 2, 2),
-    ("U", 0, 0, 2, 3),
-    ("D", "w", 2, 1),
-    ("U", 1, 0, 1, 0),
-    ("CS", 0, 0, 2),
-    ("U", 1, 0, 3, 0),
-    ("U", 0, 0, 3, 3),
-    ("U", 1, 0, 2, 0),
-    ("CS", 0, 0, 3),
-    ("Tp", 2, 2),
-    ("WQ", "w", 1, 1),
-    ("UT", 0, 0, 0),
-    ("WQ", "w", 2, 1),
-    ("D", "w", 3, 1),
-    ("U", 1, 0, 1, 1),
-    ("PP", 2, 2),
-    ("Dg", "e", 1, 0, 3),
-    ("U", 1, 0, 2, 1),
-    ("U", 1, 0, 0, 0),
-    ("U", 1, 0, 0, 1),
-    ("Dg", "e", 1, 0, 1),
-    ("U", 1, 0, 0, 2),
-    ("U", 1, 0, 2, 2),
-    ("PP", 3, 0),
-    ("UT", 0, 0, 1),
-    ("Dg", "e", 1, 0, 2),
-    ("U", 1, 0, 3, 1),
-    ("U", 1, 0, 3, 2),
-    ("SI", 0, 0, 1),
-    ("PP", 2, 1),
-    ("Dg", "e", 1, 0, 0),
-    ("UT", 0, 0, 2),
-    ("SI", 0, 0, 0),
-    ("Tp", 3, 2),
-    ("WQ", "w", 3, 1),
-    ("UT", 0, 0, 3),
-    ("SI", 0, 0, 2),
+    ("PP", 1, 3),
+    ("D", "w", 2, 0),
+    ("K", 7),
+    ("PP", 1, 1),
+    ("K", 6),
+    ("WQ", "w", 2, 0),
+    ("K", 4),
     ("Tp", 3, 1),
-    ("SI", 0, 0, 3),
-    ("XQ", 2, 0),
-    ("U", 1, 0, 0, 3),
-    ("U", 1, 0, 3, 3),
+    ("Tp", 3, 2),
+    ("XQ", 1),
+    ("D", "w", 2, 1),
+    ("Tp", 2, 0),
     ("PP", 3, 1),
-    ("CS", 1, 0, 0),
-    ("U", 1, 0, 2, 3),
-    ("U", 1, 0, 1, 2),
-    ("CS", 1, 0, 2),
-    ("U", 1, 1, 0, 0),
-    ("U", 1, 1, 0, 1),
+    ("U", 0, 0, 2, 3),
+    ("PP", 0, 2),
+    ("U", 0, 0, 3, 3),
+    ("D", "w", 3, 1),
     ("PP", 3, 2),
-    ("U", 1, 0, 1, 3),
-    ("CS", 1, 0, 3),
-    ("U", 0, 1, 0, 0),
-    ("U", 0, 1, 0, 1),
-    ("CS", 1, 0, 1),
-    ("U", 0, 1, 1, 0),
-    ("XQ", 3, 0),
-    ("U", 0, 1, 1, 1),
-    ("U", 1, 1, 1, 0),
-    ("UT", 1, 0, 0),
-    ("XQ", 2, 1),
-    ("UT", 1, 0, 2),
+    ("Tp", 2, 3),
+    ("Tp", 3, 3),
+    ("XQ", 0),
+    ("Tp", 2, 1),
+    ("CS", 0, 0, 3),
+    ("CS", 0, 0, 2),
+    ("PP", 3, 3),
+    ("U", 0, 0, 1, 3),
+    ("D", "w", 1, 1),
+    ("WQ", "w", 2, 1),
+    ("Tp", 3, 0),
+    ("U", 0, 0, 0, 3),
+    ("PP", 2, 0),
+    ("CS", 0, 0, 1),
+    ("WQ", "w", 0, 1),
+    ("Tp", 2, 2),
+    ("D", "e", 2, 0),
+    ("PP", 2, 2),
+    ("U", 1, 0, 0, 0),
+    ("U", 1, 0, 1, 0),
+    ("PP", 2, 1),
+    ("U", 1, 0, 0, 1),
+    ("CS", 0, 0, 0),
+    ("U", 1, 0, 3, 0),
+    ("D", "e", 1, 0),
+    ("C", 1, 0, 0),
+    ("U", 1, 0, 2, 0),
+    ("PP", 2, 3),
+    ("U", 1, 0, 2, 1),
+    ("UT", 0, 0, 2),
+    ("C", 1, 0, 2),
+    ("UT", 0, 0, 0),
+    ("UT", 0, 0, 1),
     ("SI", 1, 0, 0),
-    ("WQ", "e", 3, 0),
-    ("UT", 1, 0, 3),
-    ("UT", 1, 0, 1),
+    ("XQ", 2),
+    ("U", 1, 0, 1, 1),
     ("SI", 1, 0, 2),
-    ("XQ", 3, 1),
-    ("U", 0, 1, 0, 2),
-    ("SI", 1, 0, 1),
-    ("U", 0, 1, 0, 3),
+    ("U", 1, 0, 3, 1),
+    ("D", "e", 0, 0),
+    ("C", 1, 0, 1),
+    ("U", 1, 1, 1, 0),
+    ("PP", 3, 0),
+    ("U", 1, 1, 3, 0),
+    ("U", 1, 1, 2, 0),
+    ("C", 1, 0, 3),
+    ("UT", 0, 0, 3),
+    ("XQ", 3),
+    ("U", 0, 1, 1, 3),
+    ("D", "e", 3, 0),
     ("WQ", "e", 0, 0),
     ("U", 1, 1, 1, 1),
-    ("U", 1, 1, 0, 2),
-    ("CS", 0, 1, 0),
-    ("WQ", "e", 1, 0),
-    ("U", 1, 1, 0, 3),
-    ("U", 0, 1, 1, 2),
-    ("CS", 1, 1, 0),
-    ("U", 0, 1, 2, 0),
-    ("WQ", "e", 2, 0),
-    ("U", 0, 1, 2, 1),
-    ("SI", 1, 0, 3),
-    ("U", 0, 1, 3, 0),
-    ("G", 0, 0),
-    ("U", 0, 1, 1, 3),
-    ("U", 0, 1, 3, 1),
+    ("U", 1, 1, 3, 1),
+    ("C", 1, 1, 1),
+    ("U", 1, 1, 2, 1),
     ("CS", 0, 1, 1),
-    ("U", 0, 1, 3, 2),
-    ("U", 0, 1, 2, 2),
-    ("VM", 0, 3),
-    ("G", 1, 0),
-    ("U", 0, 1, 2, 3),
-    ("U", 1, 1, 1, 2),
-    ("CS", 0, 1, 2),
+    ("C", 1, 1, 3),
     ("U", 0, 1, 3, 3),
-    ("U", 1, 1, 1, 3),
+    ("SI", 1, 0, 3),
+    ("WQ", "e", 2, 0),
+    ("SI", 1, 1, 1),
+    ("U", 1, 1, 0, 0),
     ("CS", 0, 1, 3),
+    ("U", 1, 1, 0, 1),
+    ("C", 1, 1, 2),
+    ("SI", 1, 1, 3),
+    ("VM", 1, 2),
+    ("C", 1, 1, 0),
+    ("SI", 1, 0, 1),
+    ("VM", 1, 3),
+    ("SI", 1, 1, 2),
+    ("G", 1, 0),
+    ("VS", 1, 2),
+    ("VM", 1, 0),
+    ("SI", 1, 1, 0),
+    ("VS", 1, 3),
     ("VM", 1, 1),
-    ("CS", 1, 1, 1),
-    ("VX", 0, 3),
-    ("UT", 0, 1, 0),
+    ("G", 1, 1),
+    ("SI", 0, 0, 3),
+    ("VS", 1, 0),
+    ("VM", 0, 1),
+    ("VS", 1, 1),
+    ("VM", 0, 2),
+    ("SI", 0, 0, 2),
+    ("AQ", 1, 0),
+    ("SI", 0, 0, 0),
+    ("VI", 1),
+    ("VM", 0, 0),
+    ("SI", 0, 0, 1),
+    ("VM", 0, 3),
+    ("G", 0, 0),
+    ("VS", 0, 2),
+    ("VS", 0, 0),
+    ("U", 0, 1, 2, 3),
+    ("VS", 0, 1),
+    ("VS", 0, 3),
+    ("U", 0, 1, 0, 3),
+    ("VQ", 1),
+    ("CS", 0, 1, 2),
+    ("VI", 0),
+    ("CS", 0, 1, 0),
+    ("UT", 0, 1, 2),
     ("AQ", 0, 0),
+    ("UT", 0, 1, 0),
+    ("SI", 0, 1, 2),
+    ("VQ", 0),
+    ("UT", 0, 1, 3),
     ("UT", 0, 1, 1),
     ("SI", 0, 1, 0),
-    ("UT", 0, 1, 2),
-    ("AQ", 1, 0),
-    ("UT", 0, 1, 3),
-    ("SI", 0, 1, 1),
-    ("VM", 1, 3),
-    ("VX", 1, 1),
-    ("SI", 0, 1, 2),
-    ("SI", 0, 1, 3),
-    ("U", 1, 1, 2, 0),
-    ("VX", 1, 3),
-    ("U", 1, 1, 2, 1),
-    ("U", 1, 1, 2, 2),
-    ("G", 0, 1),
-    ("U", 1, 1, 2, 3),
-    ("VM", 0, 0),
-    ("CS", 1, 1, 2),
-    ("VM", 1, 0),
-    ("VX", 0, 0),
-    ("VM", 1, 2),
-    ("AQ", 0, 1),
-    ("VX", 1, 0),
-    ("U", 1, 1, 3, 0),
-    ("VX", 1, 2),
-    ("U", 1, 1, 3, 1),
-    ("VM", 0, 1),
-    ("VQ", 1),
-    ("U", 1, 1, 3, 2),
-    ("VX", 0, 1),
-    ("U", 1, 1, 3, 3),
-    ("VM", 0, 2),
-    ("CS", 1, 1, 3),
-    ("UT", 1, 1, 3),
-    ("VX", 0, 2),
-    ("UT", 1, 1, 0),
-    ("SI", 1, 1, 3),
-    ("UT", 1, 1, 2),
-    ("VQ", 0),
-    ("UT", 1, 1, 1),
-    ("SI", 1, 1, 0),
-    ("Q", 1),
-    ("SI", 1, 1, 1),
-    ("Q", 0),
-    ("SI", 1, 1, 2),
-    ("QB", 1),
-    ("Q", 2),
-    ("QB", 0),
-    ("Q", 3),
-    ("G", 1, 1),
-    ("TH", 0),
-    ("QB", 3),
     ("AQ", 1, 1),
+    ("Q", 0),
+    ("SI", 0, 1, 1),
+    ("Q", 1),
+    ("SI", 0, 1, 3),
+    ("QB", 0),
+    ("Q", 2),
+    ("QB", 1),
+    ("Q", 3),
+    ("G", 0, 1),
+    ("TH", 0),
     ("QB", 2),
+    ("AQ", 0, 1),
+    ("QB", 3),
     ("Z", 0),
-    ("Q", 6),
-    ("Q", 7),
-    ("TH", 1),
-    ("QB", 6),
-    ("Q", 5),
-    ("QB", 7),
     ("Q", 4),
-    ("QB", 5),
-    ("TH", 3),
-    ("Z", 1),
+    ("Q", 6),
+    ("TH", 1),
     ("QB", 4),
+    ("Q", 5),
+    ("QB", 6),
+    ("Q", 7),
+    ("QB", 5),
+    ("Z", 1),
+    ("QB", 7),
     ("TH", 2),
+    ("TH", 3),
     ("Z", 2),
     ("Z", 3),
 ]
@@ -290,11 +220,13 @@ def tile_pathway_latent_encoder_f5_kernel(
         xwp = ctx.enter_context(tc.tile_pool(name="xwp", bufs=2))
         xgp = ctx.enter_context(tc.tile_pool(name="xgp", bufs=2))
         yp = ctx.enter_context(tc.tile_pool(name="yp", bufs=2))
-        uyp = ctx.enter_context(tc.tile_pool(name="uyp", bufs=2))
-        grp = ctx.enter_context(tc.tile_pool(name="grp", bufs=5))
-        outs = ctx.enter_context(tc.tile_pool(name="outs", bufs=2))
+        uyp = ctx.enter_context(tc.tile_pool(name="uyp", bufs=1))
+        pairs = ctx.enter_context(tc.tile_pool(name="pairs", bufs=2))
+        grp = ctx.enter_context(tc.tile_pool(name="grp", bufs=3))
+        vlp = ctx.enter_context(tc.tile_pool(name="vlp", bufs=1))
+        outs = ctx.enter_context(tc.tile_pool(name="outs", bufs=3))
         qbp = ctx.enter_context(tc.tile_pool(name="qbp", bufs=4))
-        rawp = ctx.enter_context(tc.tile_pool(name="rawp", bufs=10))
+        rawp = ctx.enter_context(tc.tile_pool(name="rawp", bufs=8))
         ps_tr = ctx.enter_context(tc.psum_pool(name="ps_tr", bufs=TR))
         ps_mx = ctx.enter_context(tc.psum_pool(name="ps_mx", bufs=8 - TR))
         ctx.enter_context(tc.manual_schedule())
@@ -336,7 +268,9 @@ def tile_pathway_latent_encoder_f5_kernel(
         ag_t = keep.tile([P, GROUPS, 4], BF16, name="ag_t")
         lg_t = keep.tile([P, GROUPS, 4], BF16, name="lg_t")
         cf_f = keep.tile([P, TILES], F32, name="cf_f")
+        lg_f = keep.tile([P, GROUPS, 4], F32, name="lg_f")
         lb_b = keep.tile([P, H], F32, name="lb_b")
+        cf_b = keep.tile([P, CELLS], F32, name="cf_b")
         noise_t = keep.tile([P, TILES, LATENT], BF16, name="noise_t")
         nc.scalar.dma_start(out=xs_t[:], in_=x_scale.rearrange("o (g p t) -> p (o g) t", p=P, t=4))
         nc.scalar.dma_start(out=cf_c[:], in_=cell_factor.rearrange("(p i) -> p i", i=TILES))
@@ -348,17 +282,23 @@ def tile_pathway_latent_encoder_f5_kernel(
         for what in FIRST_LOADS:
             load(what)
         nc.gpsimd.tensor_copy(out=cf_f[:], in_=cf_c[:])
+        nc.gpsimd.tensor_copy(out=lg_f[:], in_=lg_t[:])
 
         xc = [keep.tile([P, PASSES, 256], U32, name=f"xc{pr}", align_bytes=64) for pr in range(4)]
         xs = [keep.tile([P, PASSES, 256], U8, name=f"xs{pr}", align_bytes=64) for pr in range(4)]
         wc = {}
         ws = {}
-        for g in range(PASSES):
-            for jg in range(GROUPS):
-                wc["w", g, jg] = keep.tile([P, 512], U32, name=f"wc{g}{jg}", align_bytes=64)
-                ws["w", g, jg] = keep.tile([P, 512], U8, name=f"ws{g}{jg}", align_bytes=64)
-            wc["e", g, 0] = keep.tile([P, H], U32, name=f"ec{g}", align_bytes=64)
-            ws["e", g, 0] = keep.tile([P, H], U8, name=f"es{g}", align_bytes=64)
+        for gp in range(2):
+            for k, jg in (("w", 0), ("w", 1), ("e", 0)):
+                wc[k, gp, jg] = keep.tile([P, 2, 512], U32, name=f"{k}c{gp}{jg}", align_bytes=64)
+                ws[k, gp, jg] = keep.tile([P, 2, 512], U8, name=f"{k}s{gp}{jg}", align_bytes=64)
+
+        def codes(k, g, jg, cols):
+            return wc[k, g // 2, jg][:, g % 2, cols].bitcast(FP8X4)
+
+        def plane(k, g, jg, cols):
+            return ws[k, g // 2, jg][:, g % 2, cols]
+
         ac = [[keep.tile([P, 512], U32, name=f"ac{jg}{h}", align_bytes=64) for h in range(HALVES)] for jg in range(GROUPS)]
         asc = [[keep.tile([P, 512], U8, name=f"asc{jg}{h}", align_bytes=64) for h in range(HALVES)] for jg in range(GROUPS)]
         vc = [keep.tile([P, H], U32, name=f"vc{jg}", align_bytes=64) for jg in range(GROUPS)]
@@ -372,6 +312,17 @@ def tile_pathway_latent_encoder_f5_kernel(
             return T[key]
 
         def CF(_):
+            for h in range(HALVES):
+                bank = get(ps_tr, "tr", ("cf", h), [P, 512], F32)
+                for i in range(4):
+                    nc.tensor.matmul(
+                        bank[:, i * P : (i + 1) * P],
+                        lhsT=cf_c[:, 4 * h + i : 4 * h + i + 1].to_broadcast([P, P]),
+                        rhs=ident_bf[:],
+                        start=True,
+                        stop=True,
+                    )
+                nc.scalar.copy(out=cf_b[:, h * 512 : (h + 1) * 512], in_=bank[:])
             bank = get(ps_tr, "tr", ("lb",), [P, 512], F32)
             for c in range(4):
                 nc.tensor.matmul(
@@ -404,54 +355,67 @@ def tile_pathway_latent_encoder_f5_kernel(
                 op=ALU.mult,
             )
 
-        def XQ(pr, k):
+        def XQ(pr):
             nc.vector.quantize_mx(
-                out=xc[pr][:, 2 * k : 2 * k + 2, :].rearrange("p g m -> p (g m)").bitcast(FP8X4),
-                scales=xs[pr][:, 2 * k : 2 * k + 2, :].rearrange("p g m -> p (g m)"),
-                in_=T["xg", pr][:, 2 * k : 2 * k + 2, :].rearrange("p g c -> p (g c)"),
+                out=xc[pr][:].rearrange("p g m -> p (g m)").bitcast(FP8X4),
+                scales=xs[pr][:].rearrange("p g m -> p (g m)"),
+                in_=T["xg", pr][:].rearrange("p g c -> p (g c)"),
             )
 
         def D(k, g, jg):
             u = (k, g, jg)
-            dst = get(grp, "gr", ("gr", u), [P, 2048], BF16, align_bytes=64)
+            both = get(pairs, "pair", ("pair", k, g // 2, jg), [P, 2, 2048], BF16, align_bytes=64)
+            dst = both[:, g % 2, :]
             if k == "w":
-                o = dst[:].rearrange("p (t m j) -> p m j t", t=4, j=4)
+                o = dst.rearrange("p (t m j) -> p m j t", t=4, j=4)
                 i = raws[u][:].rearrange("p j (m t) -> p m j t", t=4)
             else:
-                o = dst[:].rearrange("p (c i j) -> p c j i", i=4, j=4)
+                o = dst.rearrange("p (c i j) -> p c j i", i=4, j=4)
                 i = raws[u][:].rearrange("p j (c i) -> p c j i", i=4)
             if D_ENGINE[u] == "V":
                 nc.vector.tensor_copy(out=o, in_=i)
             else:
                 nc.scalar.copy(out=o, in_=i)
 
-        def Dg(k, g, jg, b):
-            u = (k, g, jg)
-            dst = get(grp, "gr", ("gr", u), [P, 2048], BF16, align_bytes=64)
-            if k == "w":
-                i = raws[u][:].rearrange("p j (m t) -> p t m j", t=4)[:, b, :, :]
-            else:
-                i = raws[u][:, :, b * P : (b + 1) * P].rearrange("p j c -> p c j")
-            nc.gpsimd.tensor_scalar(
-                out=dst[:, b * 512 : (b + 1) * 512].rearrange("p (m j) -> p m j", j=4), in0=i, scalar1=1.0, scalar2=0.0, op0=ALU.mult, op1=ALU.add
-            )
-
         def WQ(k, g, jg):
-            u = (k, g, jg)
-            nc.vector.quantize_mx(out=wc[u][:].bitcast(FP8X4), scales=ws[u][:], in_=T["gr", u][:])
-
-        def U(jg, h, k, g):
-            pr, i2 = divmod(4 * h + k, 2)
-            bank = get(ps_mx, "mx", ("u", jg, h, k), [P, 512], F32)
-            nc.tensor.matmul_mx(
-                out=bank[:],
-                lhsT=xc[pr][:, g, i2 * P : (i2 + 1) * P].bitcast(FP8X4),
-                lhsT_scale=xs[pr][:, g, i2 * P : (i2 + 1) * P],
-                rhs=wc["w", g, jg][:].bitcast(FP8X4),
-                rhs_scale=ws["w", g, jg][:],
-                start=(g == 0),
-                stop=(g == PASSES - 1),
+            u = (k, g // 2, jg)
+            nc.vector.quantize_mx(
+                out=wc[u][:].rearrange("p g c -> p (g c)").bitcast(FP8X4),
+                scales=ws[u][:].rearrange("p g c -> p (g c)"),
+                in_=T["pair", k, g // 2, jg][:].rearrange("p g c -> p (g c)"),
             )
+
+        def U(jg, h, t, k):
+            if (jg, h) in TURNED:
+                turned_u(jg, h, t)
+                return
+            col = slice(t * P, (t + 1) * P)
+            bank = get(ps_mx, "mx", ("u", jg, h, t), [P, 512], F32)
+            for g in range(PASSES):
+                nc.tensor.matmul_mx(
+                    out=bank[:, k * 256 : (k + 1) * 256],
+                    lhsT=codes("w", g, jg, col),
+                    lhsT_scale=plane("w", g, jg, col),
+                    rhs=xc[2 * h + k][:, g, :].bitcast(FP8X4),
+                    rhs_scale=xs[2 * h + k][:, g, :],
+                    start=(g == 0),
+                    stop=(g == PASSES - 1),
+                )
+
+        def turned_u(jg, h, k):
+            pr, i2 = divmod(4 * h + k, 2)
+            cells = slice(i2 * P, (i2 + 1) * P)
+            bank = get(ps_mx, "mx", ("u", jg, h, k), [P, 512], F32)
+            for g in range(PASSES):
+                nc.tensor.matmul_mx(
+                    out=bank[:],
+                    lhsT=xc[pr][:, g, cells].bitcast(FP8X4),
+                    lhsT_scale=xs[pr][:, g, cells],
+                    rhs=codes("w", g, jg, slice(0, 512)),
+                    rhs_scale=plane("w", g, jg, slice(0, 512)),
+                    start=(g == 0),
+                    stop=(g == PASSES - 1),
+                )
 
         def CS(jg, h, k):
             uy = get(uyp, "uy", ("uy", jg, h), [P, 4, 512], F32)
@@ -464,9 +428,13 @@ def tile_pathway_latent_encoder_f5_kernel(
                 nc.tensor.transpose(bank[:, k * P : (k + 1) * P], T["uy", jg, h][:, k, t * P : (t + 1) * P], ident[:])
             T["ut", jg, h, t] = bank
 
+        def C(jg, h, t):
+            y = get(yp, "y", ("y", jg, h), [P, 4, 512], F32)
+            nc.vector.tensor_tensor(out=y[:, t, :], in0=T["u", jg, h, t][:], in1=cf_b[:, h * 512 : (h + 1) * 512], op=ALU.mult)
+
         def SI(jg, h, t):
             y = get(yp, "y", ("y", jg, h), [P, 4, 512], F32)
-            nc.scalar.activation(out=y[:, t, :], in_=T["ut", jg, h, t][:], func=ACT.Silu, bias=pb_t[:, jg, t : t + 1])
+            nc.scalar.activation(out=y[:, t, :], in_=T["ut", jg, h, t][:] if (jg, h) in TURNED else y[:, t, :], func=ACT.Silu, bias=pb_t[:, jg, t : t + 1])
 
         def G(jg, h):
             dst = get(grp, "gr", ("gr", ("a", jg, h)), [P, 2048], BF16, align_bytes=64)
@@ -480,30 +448,27 @@ def tile_pathway_latent_encoder_f5_kernel(
         def AQ(jg, h):
             nc.vector.quantize_mx(out=ac[jg][h][:].bitcast(FP8X4), scales=asc[jg][h][:], in_=T["gr", ("a", jg, h)][:])
 
-        def VM(jg, c):
-            cols = slice(c * P, (c + 1) * P)
-            bank = get(ps_mx, "mx", ("v", jg, c), [P, 512], F32)
-            for t in range(4):
-                col = slice(t * P, (t + 1) * P)
-                for g in range(PASSES):
-                    nc.tensor.matmul_mx(
-                        out=bank[:, t * P : (t + 1) * P],
-                        lhsT=wc["w", g, jg][:, col].bitcast(FP8X4),
-                        lhsT_scale=ws["w", g, jg][:, col],
-                        rhs=wc["e", g, 0][:, cols].bitcast(FP8X4),
-                        rhs_scale=ws["e", g, 0][:, cols],
-                        start=(g == 0),
-                        stop=(g == PASSES - 1),
-                    )
+        def VM(jg, t):
+            col = slice(t * P, (t + 1) * P)
+            bank = get(ps_mx, "mx", ("v", jg, t), [P, 512], F32)
+            for g in range(PASSES):
+                nc.tensor.matmul_mx(
+                    out=bank[:],
+                    lhsT=codes("w", g, jg, col),
+                    lhsT_scale=plane("w", g, jg, col),
+                    rhs=codes("e", g, 0, slice(0, 512)),
+                    rhs_scale=plane("e", g, 0, slice(0, 512)),
+                    start=(g == 0),
+                    stop=(g == PASSES - 1),
+                )
 
-        def VX(jg, c):
+        def VS(jg, t):
+            vl = get(vlp, "vl", ("vl", jg), [P, 4, 512], BF16)
+            nc.scalar.activation(out=vl[:, t, :], in_=T["v", jg, t][:], func=ACT.Copy, scale=lg_f[:, jg, t : t + 1])
+
+        def VI(jg):
             dst = get(grp, "gr", ("gr", ("v", jg)), [P, 2048], BF16, align_bytes=64)
-            nc.vector.tensor_tensor(
-                out=dst[:, c * 512 : (c + 1) * 512].rearrange("p (n t) -> p n t", t=4),
-                in0=T["v", jg, c][:].rearrange("p (t n) -> p n t", t=4),
-                in1=lg_t[:, jg, :].unsqueeze(1).to_broadcast([P, P, 4]),
-                op=ALU.mult,
-            )
+            nc.vector.tensor_copy(out=dst[:].rearrange("p (c i t) -> p c t i", i=4, t=4), in_=T["vl", jg][:].rearrange("p t (c i) -> p c t i", i=4))
 
         def VQ(jg):
             nc.vector.quantize_mx(out=vc[jg][:].bitcast(FP8X4), scales=vsc[jg][:], in_=T["gr", ("v", jg)][:])
@@ -549,6 +514,6 @@ def tile_pathway_latent_encoder_f5_kernel(
             eng.tensor_tensor(out=z[:], in0=z[:], in1=T["qb", pr][:, :, 0:LATENT], op=ALU.add)
             nc.sync.dma_start(out=z_rows[:, rows, :], in_=z[:])
 
-        steps = dict(CF=CF, Dg=Dg, K=K, Tp=Tp, PP=PP, XQ=XQ, D=D, WQ=WQ, U=U, SI=SI, G=G, AQ=AQ, CS=CS, UT=UT, VM=VM, VX=VX, VQ=VQ, Q=Q, QB=QB, TH=TH, Z=Z)
+        steps = dict(C=C, CF=CF, K=K, Tp=Tp, PP=PP, XQ=XQ, D=D, WQ=WQ, U=U, SI=SI, G=G, AQ=AQ, CS=CS, UT=UT, VM=VM, VS=VS, VI=VI, VQ=VQ, Q=Q, QB=QB, TH=TH, Z=Z)
         for step in ORDER:
             steps[step[0]](*step[1:])

from contextlib import ExitStack

import concourse.mybir as mybir
from concourse.masks import make_identity

F32 = mybir.dt.float32
BF16 = mybir.dt.bfloat16
U32 = mybir.dt.uint32
U8 = mybir.dt.uint8
F8 = mybir.dt.float8_e4m3fn
FP8X4 = mybir.dt.float8_e4m3fn_x4
ACT = mybir.ActivationFunctionType
ALU = mybir.AluOpType

CELLS, GENES, PATHWAYS, LATENT = 1024, 2048, 1024, 256
H = 2 * LATENT
P = 128
PASSES = GENES // 512
GROUPS = PATHWAYS // 512
HALVES = CELLS // 512
TILES = CELLS // P
TR = 4
TURNED = {(0, 0), (0, 1)}
Z_ON_GPSIMD = (0, 1,)
D_ENGINE = {("w", 0, 0): "V", ("w", 1, 0): "V", ("w", 2, 0): "V", ("w", 3, 0): "S", ("w", 0, 1): "S", ("w", 1, 1): "S", ("w", 2, 1): "S", ("w", 3, 1): "S", ("e", 0, 0): "S", ("e", 1, 0): "S", ("e", 2, 0): "S", ("e", 3, 0): "S"}
FIRST_LOADS = ("x0", "w00", "w10", "x1", "w20", "w30", "w01", "x2", "w11", "w21",)
LOADS_AFTER = {0: ("x3", "w31",), 3: ("e2", "e0",), 4: ("e3", "noise",), 5: ("e1",)}
FLOPS = 2 * CELLS * GENES * PATHWAYS + 2 * GENES * PATHWAYS * H + 2 * CELLS * PATHWAYS * H

ORDER = [
    ("K", 1),
    ("D", "w", 0, 0),
    ("K", 0),
    ("CF", 0),
    ("Tp", 0, 1),
    ("D", "w", 1, 0),
    ("Tp", 0, 0),
    ("Tp", 0, 3),
    ("PP", 0, 1),
    ("K", 3),
    ("Tp", 0, 2),
    ("WQ", "w", 0, 0),
    ("K", 2),
    ("PP", 0, 0),
    ("D", "w", 3, 0),
    ("Tp", 1, 1),
    ("PP", 0, 3),
    ("Tp", 1, 2),
    ("PP", 1, 2),
    ("Tp", 1, 0),
    ("K", 5),
    ("PP", 1, 0),
    ("Tp", 1, 3),
    ("D", "w", 0, 1),
    ("PP", 1, 3),
    ("D", "w", 2, 0),
    ("K", 7),
    ("PP", 1, 1),
    ("K", 6),
    ("WQ", "w", 2, 0),
    ("K", 4),
    ("Tp", 3, 1),
    ("Tp", 3, 2),
    ("XQ", 1),
    ("D", "w", 2, 1),
    ("Tp", 2, 0),
    ("PP", 3, 1),
    ("U", 0, 0, 2, 3),
    ("PP", 0, 2),
    ("U", 0, 0, 3, 3),
    ("D", "w", 3, 1),
    ("PP", 3, 2),
    ("Tp", 2, 3),
    ("Tp", 3, 3),
    ("XQ", 0),
    ("Tp", 2, 1),
    ("CS", 0, 0, 3),
    ("CS", 0, 0, 2),
    ("PP", 3, 3),
    ("U", 0, 0, 1, 3),
    ("D", "w", 1, 1),
    ("WQ", "w", 2, 1),
    ("Tp", 3, 0),
    ("U", 0, 0, 0, 3),
    ("PP", 2, 0),
    ("CS", 0, 0, 1),
    ("WQ", "w", 0, 1),
    ("Tp", 2, 2),
    ("D", "e", 2, 0),
    ("PP", 2, 2),
    ("U", 1, 0, 0, 0),
    ("U", 1, 0, 1, 0),
    ("PP", 2, 1),
    ("U", 1, 0, 0, 1),
    ("CS", 0, 0, 0),
    ("U", 1, 0, 3, 0),
    ("D", "e", 1, 0),
    ("C", 1, 0, 0),
    ("U", 1, 0, 2, 0),
    ("PP", 2, 3),
    ("U", 1, 0, 2, 1),
    ("UT", 0, 0, 2),
    ("C", 1, 0, 2),
    ("UT", 0, 0, 0),
    ("UT", 0, 0, 1),
    ("SI", 1, 0, 0),
    ("XQ", 2),
    ("U", 1, 0, 1, 1),
    ("SI", 1, 0, 2),
    ("U", 1, 0, 3, 1),
    ("D", "e", 0, 0),
    ("C", 1, 0, 1),
    ("U", 1, 1, 1, 0),
    ("PP", 3, 0),
    ("U", 1, 1, 3, 0),
    ("U", 1, 1, 2, 0),
    ("C", 1, 0, 3),
    ("UT", 0, 0, 3),
    ("XQ", 3),
    ("U", 0, 1, 1, 3),
    ("D", "e", 3, 0),
    ("WQ", "e", 0, 0),
    ("U", 1, 1, 1, 1),
    ("U", 1, 1, 3, 1),
    ("C", 1, 1, 1),
    ("U", 1, 1, 2, 1),
    ("CS", 0, 1, 1),
    ("C", 1, 1, 3),
    ("U", 0, 1, 3, 3),
    ("SI", 1, 0, 3),
    ("WQ", "e", 2, 0),
    ("SI", 1, 1, 1),
    ("U", 1, 1, 0, 0),
    ("CS", 0, 1, 3),
    ("U", 1, 1, 0, 1),
    ("C", 1, 1, 2),
    ("SI", 1, 1, 3),
    ("VM", 1, 2),
    ("C", 1, 1, 0),
    ("SI", 1, 0, 1),
    ("VM", 1, 3),
    ("SI", 1, 1, 2),
    ("G", 1, 0),
    ("VS", 1, 2),
    ("VM", 1, 0),
    ("SI", 1, 1, 0),
    ("VS", 1, 3),
    ("VM", 1, 1),
    ("G", 1, 1),
    ("SI", 0, 0, 3),
    ("VS", 1, 0),
    ("VM", 0, 1),
    ("VS", 1, 1),
    ("VM", 0, 2),
    ("SI", 0, 0, 2),
    ("AQ", 1, 0),
    ("SI", 0, 0, 0),
    ("VI", 1),
    ("VM", 0, 0),
    ("SI", 0, 0, 1),
    ("VM", 0, 3),
    ("G", 0, 0),
    ("VS", 0, 2),
    ("VS", 0, 0),
    ("U", 0, 1, 2, 3),
    ("VS", 0, 1),
    ("VS", 0, 3),
    ("U", 0, 1, 0, 3),
    ("VQ", 1),
    ("CS", 0, 1, 2),
    ("VI", 0),
    ("CS", 0, 1, 0),
    ("UT", 0, 1, 2),
    ("AQ", 0, 0),
    ("UT", 0, 1, 0),
    ("SI", 0, 1, 2),
    ("VQ", 0),
    ("UT", 0, 1, 3),
    ("UT", 0, 1, 1),
    ("SI", 0, 1, 0),
    ("AQ", 1, 1),
    ("Q", 0),
    ("SI", 0, 1, 1),
    ("Q", 1),
    ("SI", 0, 1, 3),
    ("QB", 0),
    ("Q", 2),
    ("QB", 1),
    ("Q", 3),
    ("G", 0, 1),
    ("TH", 0),
    ("QB", 2),
    ("AQ", 0, 1),
    ("QB", 3),
    ("Z", 0),
    ("Q", 4),
    ("Q", 6),
    ("TH", 1),
    ("QB", 4),
    ("Q", 5),
    ("QB", 6),
    ("Q", 7),
    ("QB", 5),
    ("Z", 1),
    ("QB", 7),
    ("TH", 2),
    ("TH", 3),
    ("Z", 2),
    ("Z", 3),
]


def tile_pathway_latent_encoder_f5_kernel(
    tc, x_bytes, x_scale, w, e, cell_factor, pathway_bias, activity_gain, loading_gain, latent_bias, noise, mu_out, sd_out, z_out
):
    nc = tc.nc
    with ExitStack() as ctx:
        keep = ctx.enter_context(tc.tile_pool(name="keep", bufs=1))
        xin = ctx.enter_context(tc.tile_pool(name="xin", bufs=3))
        xwp = ctx.enter_context(tc.tile_pool(name="xwp", bufs=2))
        xgp = ctx.enter_context(tc.tile_pool(name="xgp", bufs=2))
        yp = ctx.enter_context(tc.tile_pool(name="yp", bufs=2))
        uyp = ctx.enter_context(tc.tile_pool(name="uyp", bufs=1))
        pairs = ctx.enter_context(tc.tile_pool(name="pairs", bufs=2))
        grp = ctx.enter_context(tc.tile_pool(name="grp", bufs=3))
        vlp = ctx.enter_context(tc.tile_pool(name="vlp", bufs=1))
        outs = ctx.enter_context(tc.tile_pool(name="outs", bufs=3))
        qbp = ctx.enter_context(tc.tile_pool(name="qbp", bufs=4))
        rawp = ctx.enter_context(tc.tile_pool(name="rawp", bufs=8))
        ps_tr = ctx.enter_context(tc.psum_pool(name="ps_tr", bufs=TR))
        ps_mx = ctx.enter_context(tc.psum_pool(name="ps_mx", bufs=8 - TR))
        ctx.enter_context(tc.manual_schedule())

        x_raw = {}
        raws = {}
        x_rows = x_bytes.rearrange("(p i) k -> p i k", i=TILES)

        def load(what):
            kind = what[0]
            if kind == "x":
                pr = int(what[1])
                x_raw[pr] = xin.tile([P, 2, GENES], U8, name="x_raw")
                nc.sync.dma_start(out=x_raw[pr][:], in_=x_rows[:, 2 * pr : 2 * pr + 2, :])
            elif kind == "w":
                g, jg = int(what[1]), int(what[2])
                raws["w", g, jg] = rawp.tile([P, 4, 512], BF16, name="raw")
                nc.sync.dma_start(
                    out=raws["w", g, jg][:], in_=w[g * 512 : (g + 1) * 512, jg * 512 : (jg + 1) * 512].rearrange("(p j) n -> p j n", j=4)
                )
            elif kind == "e":
                g = int(what[1])
                raws["e", g, 0] = rawp.tile([P, 4, H], BF16, name="raw")
                nc.sync.dma_start(out=raws["e", g, 0][:], in_=e[g * 512 : (g + 1) * 512, :].rearrange("(p j) n -> p j n", j=4))
            else:
                nc.sync.dma_start(out=noise_t[:], in_=noise.rearrange("(p i) l -> p i l", i=TILES))

        warm = keep.tile([P, 1], F32, name="warm")
        nc.gpsimd.memset(warm[:], 0.0)
        ident_bf = keep.tile([P, P], BF16, name="ident_bf")
        make_identity(nc, ident_bf[:])
        ident = keep.tile([P, P], F32, name="ident")
        make_identity(nc, ident[:])

        xs_t = keep.tile([P, PASSES, 4], F32, name="xs_t")
        cf_c = keep.tile([P, TILES], BF16, name="cf_c")
        lb_c = keep.tile([P, 4], BF16, name="lb_c")
        pb_t = keep.tile([P, GROUPS, 4], BF16, name="pb_t")
        ag_t = keep.tile([P, GROUPS, 4], BF16, name="ag_t")
        lg_t = keep.tile([P, GROUPS, 4], BF16, name="lg_t")
        cf_f = keep.tile([P, TILES], F32, name="cf_f")
        lg_f = keep.tile([P, GROUPS, 4], F32, name="lg_f")
        lb_b = keep.tile([P, H], F32, name="lb_b")
        cf_b = keep.tile([P, CELLS], F32, name="cf_b")
        noise_t = keep.tile([P, TILES, LATENT], BF16, name="noise_t")
        nc.scalar.dma_start(out=xs_t[:], in_=x_scale.rearrange("o (g p t) -> p (o g) t", p=P, t=4))
        nc.scalar.dma_start(out=cf_c[:], in_=cell_factor.rearrange("(p i) -> p i", i=TILES))
        nc.scalar.dma_start(out=lb_c[:], in_=latent_bias.rearrange("(n c) -> n c", c=4))
        nc.scalar.dma_start(out=pb_t[:], in_=pathway_bias.rearrange("(g p t) -> p g t", p=P, t=4))
        nc.scalar.dma_start(out=ag_t[:], in_=activity_gain.rearrange("(g p t) -> p g t", p=P, t=4))
        nc.scalar.dma_start(out=lg_t[:], in_=loading_gain.rearrange("(g p t) -> p g t", p=P, t=4))
        nc.scalar.activation(out=warm[:], in_=warm[:], func=ACT.Silu)
        for what in FIRST_LOADS:
            load(what)
        nc.gpsimd.tensor_copy(out=cf_f[:], in_=cf_c[:])
        nc.gpsimd.tensor_copy(out=lg_f[:], in_=lg_t[:])

        xc = [keep.tile([P, PASSES, 256], U32, name=f"xc{pr}", align_bytes=64) for pr in range(4)]
        xs = [keep.tile([P, PASSES, 256], U8, name=f"xs{pr}", align_bytes=64) for pr in range(4)]
        wc = {}
        ws = {}
        for gp in range(2):
            for k, jg in (("w", 0), ("w", 1), ("e", 0)):
                wc[k, gp, jg] = keep.tile([P, 2, 512], U32, name=f"{k}c{gp}{jg}", align_bytes=64)
                ws[k, gp, jg] = keep.tile([P, 2, 512], U8, name=f"{k}s{gp}{jg}", align_bytes=64)

        def codes(k, g, jg, cols):
            return wc[k, g // 2, jg][:, g % 2, cols].bitcast(FP8X4)

        def plane(k, g, jg, cols):
            return ws[k, g // 2, jg][:, g % 2, cols]

        ac = [[keep.tile([P, 512], U32, name=f"ac{jg}{h}", align_bytes=64) for h in range(HALVES)] for jg in range(GROUPS)]
        asc = [[keep.tile([P, 512], U8, name=f"asc{jg}{h}", align_bytes=64) for h in range(HALVES)] for jg in range(GROUPS)]
        vc = [keep.tile([P, H], U32, name=f"vc{jg}", align_bytes=64) for jg in range(GROUPS)]
        vsc = [keep.tile([P, H], U8, name=f"vsc{jg}", align_bytes=64) for jg in range(GROUPS)]

        T = {}

        def get(pool, tag, key, shape, dt, **kw):
            if key not in T:
                T[key] = pool.tile(shape, dt, name=tag, **kw)
            return T[key]

        def CF(_):
            for h in range(HALVES):
                bank = get(ps_tr, "tr", ("cf", h), [P, 512], F32)
                for i in range(4):
                    nc.tensor.matmul(
                        bank[:, i * P : (i + 1) * P],
                        lhsT=cf_c[:, 4 * h + i : 4 * h + i + 1].to_broadcast([P, P]),
                        rhs=ident_bf[:],
                        start=True,
                        stop=True,
                    )
                nc.scalar.copy(out=cf_b[:, h * 512 : (h + 1) * 512], in_=bank[:])
            bank = get(ps_tr, "tr", ("lb",), [P, 512], F32)
            for c in range(4):
                nc.tensor.matmul(
                    bank[:, c * P : (c + 1) * P], lhsT=lb_c[:, c : c + 1].to_broadcast([P, P]), rhs=ident_bf[:], start=True, stop=True
                )
            nc.scalar.copy(out=lb_b[:].rearrange("p (n c) -> p n c", c=4), in_=bank[:].rearrange("p (c n) -> p n c", c=4))

        def K(i):
            pr, i2 = divmod(i, 2)
            xw = get(xwp, "xw", ("xw", pr), [P, 2, GENES], BF16)
            nc.scalar.copy(out=xw[:, i2, :], in_=x_raw[pr][:, i2, :].bitcast(F8))
            for what in LOADS_AFTER.get(i, ()):
                load(what)

        def Tp(pr, g):
            bank = get(ps_tr, "tr", ("x", pr, g), [P, 512], F32)
            for i2 in range(2):
                words = T["xw", pr][:, i2, :].bitcast(F32)
                for u in range(2):
                    nc.tensor.transpose(
                        bank[:, u * 256 + i2 * P : u * 256 + (i2 + 1) * P], words[:, 256 * g + u : 256 * (g + 1) : 2], ident[:]
                    )

        def PP(pr, g):
            xg = get(xgp, "xg", ("xg", pr), [P, PASSES, 1024], BF16, align_bytes=64)
            nc.vector.tensor_tensor(
                out=xg[:, g, :].rearrange("p (m u e) -> p m u e", u=2, e=2),
                in0=T["x", pr, g][:].bitcast(BF16).rearrange("p (u m e) -> p m u e", u=2, e=2),
                in1=xs_t[:, g, :].rearrange("p (u e) -> p u e", e=2).unsqueeze(1).to_broadcast([P, 256, 2, 2]),
                op=ALU.mult,
            )

        def XQ(pr):
            nc.vector.quantize_mx(
                out=xc[pr][:].rearrange("p g m -> p (g m)").bitcast(FP8X4),
                scales=xs[pr][:].rearrange("p g m -> p (g m)"),
                in_=T["xg", pr][:].rearrange("p g c -> p (g c)"),
            )

        def D(k, g, jg):
            u = (k, g, jg)
            both = get(pairs, "pair", ("pair", k, g // 2, jg), [P, 2, 2048], BF16, align_bytes=64)
            dst = both[:, g % 2, :]
            if k == "w":
                o = dst.rearrange("p (t m j) -> p m j t", t=4, j=4)
                i = raws[u][:].rearrange("p j (m t) -> p m j t", t=4)
            else:
                o = dst.rearrange("p (c i j) -> p c j i", i=4, j=4)
                i = raws[u][:].rearrange("p j (c i) -> p c j i", i=4)
            if D_ENGINE[u] == "V":
                nc.vector.tensor_copy(out=o, in_=i)
            else:
                nc.scalar.copy(out=o, in_=i)

        def WQ(k, g, jg):
            u = (k, g // 2, jg)
            nc.vector.quantize_mx(
                out=wc[u][:].rearrange("p g c -> p (g c)").bitcast(FP8X4),
                scales=ws[u][:].rearrange("p g c -> p (g c)"),
                in_=T["pair", k, g // 2, jg][:].rearrange("p g c -> p (g c)"),
            )

        def U(jg, h, t, k):
            if (jg, h) in TURNED:
                turned_u(jg, h, t)
                return
            col = slice(t * P, (t + 1) * P)
            bank = get(ps_mx, "mx", ("u", jg, h, t), [P, 512], F32)
            for g in range(PASSES):
                nc.tensor.matmul_mx(
                    out=bank[:, k * 256 : (k + 1) * 256],
                    lhsT=codes("w", g, jg, col),
                    lhsT_scale=plane("w", g, jg, col),
                    rhs=xc[2 * h + k][:, g, :].bitcast(FP8X4),
                    rhs_scale=xs[2 * h + k][:, g, :],
                    start=(g == 0),
                    stop=(g == PASSES - 1),
                )

        def turned_u(jg, h, k):
            pr, i2 = divmod(4 * h + k, 2)
            cells = slice(i2 * P, (i2 + 1) * P)
            bank = get(ps_mx, "mx", ("u", jg, h, k), [P, 512], F32)
            for g in range(PASSES):
                nc.tensor.matmul_mx(
                    out=bank[:],
                    lhsT=xc[pr][:, g, cells].bitcast(FP8X4),
                    lhsT_scale=xs[pr][:, g, cells],
                    rhs=codes("w", g, jg, slice(0, 512)),
                    rhs_scale=plane("w", g, jg, slice(0, 512)),
                    start=(g == 0),
                    stop=(g == PASSES - 1),
                )

        def CS(jg, h, k):
            uy = get(uyp, "uy", ("uy", jg, h), [P, 4, 512], F32)
            i = 4 * h + k
            nc.scalar.activation(out=uy[:, k, :], in_=T["u", jg, h, k][:], func=ACT.Copy, scale=cf_f[:, i : i + 1])

        def UT(jg, h, t):
            bank = get(ps_tr, "tr", ("y", jg, h, t), [P, 512], F32)
            for k in range(4):
                nc.tensor.transpose(bank[:, k * P : (k + 1) * P], T["uy", jg, h][:, k, t * P : (t + 1) * P], ident[:])
            T["ut", jg, h, t] = bank

        def C(jg, h, t):
            y = get(yp, "y", ("y", jg, h), [P, 4, 512], F32)
            nc.vector.tensor_tensor(out=y[:, t, :], in0=T["u", jg, h, t][:], in1=cf_b[:, h * 512 : (h + 1) * 512], op=ALU.mult)

        def SI(jg, h, t):
            y = get(yp, "y", ("y", jg, h), [P, 4, 512], F32)
            nc.scalar.activation(out=y[:, t, :], in_=T["ut", jg, h, t][:] if (jg, h) in TURNED else y[:, t, :], func=ACT.Silu, bias=pb_t[:, jg, t : t + 1])

        def G(jg, h):
            dst = get(grp, "gr", ("gr", ("a", jg, h)), [P, 2048], BF16, align_bytes=64)
            nc.vector.tensor_tensor(
                out=dst[:].rearrange("p (c i t) -> p c t i", i=4, t=4),
                in0=T["y", jg, h][:].rearrange("p t (c i) -> p c t i", i=4),
                in1=ag_t[:, jg, :].unsqueeze(1).unsqueeze(3).to_broadcast([P, P, 4, 4]),
                op=ALU.mult,
            )

        def AQ(jg, h):
            nc.vector.quantize_mx(out=ac[jg][h][:].bitcast(FP8X4), scales=asc[jg][h][:], in_=T["gr", ("a", jg, h)][:])

        def VM(jg, t):
            col = slice(t * P, (t + 1) * P)
            bank = get(ps_mx, "mx", ("v", jg, t), [P, 512], F32)
            for g in range(PASSES):
                nc.tensor.matmul_mx(
                    out=bank[:],
                    lhsT=codes("w", g, jg, col),
                    lhsT_scale=plane("w", g, jg, col),
                    rhs=codes("e", g, 0, slice(0, 512)),
                    rhs_scale=plane("e", g, 0, slice(0, 512)),
                    start=(g == 0),
                    stop=(g == PASSES - 1),
                )

        def VS(jg, t):
            vl = get(vlp, "vl", ("vl", jg), [P, 4, 512], BF16)
            nc.scalar.activation(out=vl[:, t, :], in_=T["v", jg, t][:], func=ACT.Copy, scale=lg_f[:, jg, t : t + 1])

        def VI(jg):
            dst = get(grp, "gr", ("gr", ("v", jg)), [P, 2048], BF16, align_bytes=64)
            nc.vector.tensor_copy(out=dst[:].rearrange("p (c i t) -> p c t i", i=4, t=4), in_=T["vl", jg][:].rearrange("p t (c i) -> p c t i", i=4))

        def VQ(jg):
            nc.vector.quantize_mx(out=vc[jg][:].bitcast(FP8X4), scales=vsc[jg][:], in_=T["gr", ("v", jg)][:])

        def Q(i):
            h, k = divmod(i, 4)
            cells = slice(k * P, (k + 1) * P)
            bank = get(ps_mx, "mx", ("q", i), [P, 512], F32)
            for jg in range(GROUPS):
                nc.tensor.matmul_mx(
                    out=bank[:],
                    lhsT=ac[jg][h][:, cells].bitcast(FP8X4),
                    lhsT_scale=asc[jg][h][:, cells],
                    rhs=vc[jg][:].bitcast(FP8X4),
                    rhs_scale=vsc[jg][:],
                    start=(jg == 0),
                    stop=(jg == GROUPS - 1),
                )

        mu_rows = mu_out.rearrange("(p i) l -> p i l", i=TILES)
        sd_rows = sd_out.rearrange("(p i) l -> p i l", i=TILES)
        z_rows = z_out.rearrange("(p i) l -> p i l", i=TILES)

        def QB(i):
            pr, i2 = divmod(i, 2)
            qb = get(qbp, "qb", ("qb", pr), [P, 2, H], F32)
            nc.vector.tensor_tensor(out=qb[:, i2, :], in0=T["q", i][:], in1=lb_b[:], op=ALU.add)

        def TH(pr):
            qb = T["qb", pr]
            rows = slice(2 * pr, 2 * pr + 2)
            nc.sync.dma_start(out=mu_rows[:, rows, :], in_=qb[:, :, 0:LATENT])
            sd = get(outs, "sd", ("sd", pr), [P, 2, LATENT], F32)
            nc.scalar.activation(out=sd[:], in_=qb[:, :, LATENT:H], func=ACT.Tanh)
            nc.scalar.activation(out=sd[:], in_=sd[:], func=ACT.Exp, scale=0.5)
            nc.sync.dma_start(out=sd_rows[:, rows, :], in_=sd[:])

        def Z(pr):
            rows = slice(2 * pr, 2 * pr + 2)
            z = get(outs, "z", ("z", pr), [P, 2, LATENT], F32)
            eng = nc.gpsimd if pr in Z_ON_GPSIMD else nc.vector
            eng.tensor_tensor(out=z[:], in0=T["sd", pr][:], in1=noise_t[:, rows, :], op=ALU.mult)
            eng.tensor_tensor(out=z[:], in0=z[:], in1=T["qb", pr][:, :, 0:LATENT], op=ALU.add)
            nc.sync.dma_start(out=z_rows[:, rows, :], in_=z[:])

        steps = dict(C=C, CF=CF, K=K, Tp=Tp, PP=PP, XQ=XQ, D=D, WQ=WQ, U=U, SI=SI, G=G, AQ=AQ, CS=CS, UT=UT, VM=VM, VS=VS, VI=VI, VQ=VQ, Q=Q, QB=QB, TH=TH, Z=Z)
        for step in ORDER:
            steps[step[0]](*step[1:])
